import numpy as np, ml_dtypes
CORES = [35,38,43,46]
N = 4
import mx_ref
BF = ml_dtypes.bfloat16
def gcols(t, e):
    v = np.concatenate([t.reshape(8, 16, -1, 4), np.zeros((8, 16, 1, 4), BF)], axis=2)
    return np.ascontiguousarray(np.stack([v[g][:, e[g]] for g in range(8)])).reshape(128, -1)
def tile(rs):
    return np.stack(rs, axis=2).reshape(128, -1).astype(BF)
def pick(q, e):
    c = np.concatenate([q[0].reshape(128, -1, 4), np.zeros((128, 1, 4), np.uint8)], axis=1); s = np.concatenate([q[1], np.ones((16, 1), np.uint8)], axis=1)
    return (np.ascontiguousarray(c[:, e].reshape(128, -1)), np.ascontiguousarray(s[:, e]))
def join(*qs):
    return (np.concatenate([q[0] for q in qs], axis=1), np.concatenate([q[1] for q in qs], axis=1))
def put(q, e, v):
    c, s = q[0].reshape(128, -1, 4).copy(), q[1].copy(); c[:, e] = v[0].reshape(128, -1, 4); s[:, e] = v[1]
    return (c.reshape(128, -1), s)
def pk(c, s):
    return (np.ascontiguousarray(c), mx_ref.live(s))
def emit(q):
    return q[0], q[1]
def packed(v, rng):
    q = [mx_ref.quantize(np.ascontiguousarray(v[r])) for r in range(N)]
    return np.stack([a for a, b in q]), np.stack([mx_ref.plane(b, rng) for a, b in q])
def f(rng, *shape):
    return mx_ref.flush((rng.standard_normal(shape, dtype=np.float32) * np.exp2(rng.integers(-2, 3, shape[:-1] + (1,)))).astype(BF))
def wide(rng, *shape, cols=0):
    v = rng.standard_normal(shape, dtype=np.float32) * np.exp2(rng.integers(-12, 13, shape)).astype(np.float32)
    if cols: v *= np.repeat(np.exp2(rng.integers(-cols, cols + 1, shape[:-2] + (1, shape[-1] // 4))) * (rng.random(shape[:-2] + (1, shape[-1] // 4)) > 0.0625), 4, axis=-1).astype(np.float32)
    return mx_ref.flush(v.astype(BF))
C, K, R = 224, 28, 3
STEP = [3, 1, 2]
def runs(p):
    here, beside = [], []
    for g in range(8):
        a, s = p[16 * g] + np.float32(0.0), p[16 * g + 1] + np.float32(0.0)
        b = np.append(0, np.sort(1 + np.argsort(-s[1:], kind="stable")[:K - 1]))
        n = np.diff(np.append(b, C))
        e = []
        for i in range(K):
            k = b[i] + np.argsort(-a[b[i]:b[i] + n[i]], kind="stable")[:2]
            e += [(-a[k[0]], k[0], 0, i), (-a[k[-1]], k[-1], 1, i)]
        e = [(q[1], b[q[3]], n[q[3]]) for q in sorted(e)]
        h, m = [], []
        for (k, i, l), (k2, i2, l2) in zip(e, e[1:] + e[:1]):
            o = np.arange(l)
            h.append(i + (k - i + o) % l)
            m.append(i2 + (k2 - i2 + o) % l2)
        here.append(np.concatenate(h))
        beside.append(np.concatenate(m))
    return np.stack(here), np.stack(beside)
def big(v):
    v = v.astype(np.float32)
    v[np.abs(v) < np.float32(2.0 ** -16)] = 0
    return v.astype(BF)
def numbers_of(rng):
    return {"x": big(f(rng, N, 128, 4 * C)), "u": np.array(f(rng, N, 128, 512)), "v": np.array(f(rng, N, 128, 512))}
def weights(rng, still=[]):
    w = np.array(f(rng, N, 128, 2048)).reshape(N, 8, 16, 4, 8, 16, 4)
    for i in still:
        w[:, :, i] = 0
        w[:, :, :, :, :, i] = 0
    c, p = packed(w.reshape(N, 128, 2048), rng)
    return {"wc": c, "ws": p}
def signs(rng):
    return np.stack([rng.permutation(8) % 2 * 2.0 - 1.0 for r in range(N)])
def setup_inputs(rng):
    return {**numbers_of(rng), **weights(rng)}
def setup_inputs_ties(rng):
    d = numbers_of(rng)
    e = rng.permutation(N)
    x = d["x"].reshape(N, 8, 16, C, 4)
    for r in range(N):
        k = np.zeros(C, int) if r == e[0] else rng.permutation(C) % 3
        a = x[r][:, :8, :3].copy()
        a[:, :, 2] = 0
        x[r][:, :8] = a[:, :, k]
    x[e[1]] = 0
    u = d["u"].reshape(N, 8, 16, 8, 16, 4)
    k = u.copy()
    u[:, :, :, :, :2] = 0
    for g in range(8): u[:, g, :8, g, :2] = k[:, g, :8, g, :2]
    return {"x": x.reshape(N, 128, 4 * C), "u": u.reshape(N, 128, 512), "v": d["v"], **weights(rng, range(8))}
def setup_inputs_near(rng):
    d = numbers_of(rng)
    x = np.zeros((N, 8, 16, C, 4), np.float32)
    u = d["u"].reshape(N, 128, 128, 4)
    u[:, :, ::16] = 0
    u[:, :, 1::16] = 0
    kind, c = rng.permutation(N) % 4, [signs(rng), signs(rng)]
    j = np.arange(C)
    for r in range(N):
        size = 1.0 if kind[r] < 2 else 2.0 ** -4
        k = 1.0 if kind[r] == 0 else 2.0 ** -30
        l = C // 2 if kind[r] == 3 else C
        for row in range(2):
            if row == 0: i = (j + rng.integers(0, C, (8, 1))) % l
            else:
                i = (j + 8 * rng.integers(0, C // 8, (8, 1))) % l
                i = i % 8 * (l // 8) + i // 8
            s = i if kind[r] == 3 else (i + 1 - row) // 2
            z = ((s[:, :, None] >> np.arange(8)) & 1) * np.exp2(np.arange(8) - 23.0) * size
            if kind[r] < 2:
                x[r, :, row, :, 0] = c[row][r][:, None]
                for g in rng.permutation(8)[:4]: x[r, g, row, rng.integers(1, C), 0] *= np.float32(2.0 ** 30)
            if kind[r] == 3: x[r, :, row, :, 0] = (8 + j // (C // 2)) * 2.0 ** -30
            x[r, :, 8 + 2 * row] = z[:, :, :4]
            x[r, :, 9 + 2 * row] = z[:, :, 4:]
            for h in range(0, 128, 16):
                u[r, h + row, h + row, 0] = k
                u[r, h + 8 + 2 * row:h + 10 + 2 * row, h + row] = k
        x[r, :, 12:] = rng.integers(4, 8, (8, 4, C, 4)) * 2.0 ** -20 * size
    return {"x": x.reshape(N, 128, 4 * C).astype(BF), "u": u.reshape(N, 128, 512), "v": d["v"], **weights(rng, range(12))}
def setup_inputs_huge(rng):
    d = numbers_of(rng)
    c = np.stack([rng.permutation(C) % 2 * 2.0 - 1.0 for r in range(N)])
    c[rng.permutation(N) < N // 2] = -1
    x = 2.0 ** 30 * (0.6 + 0.2 * rng.random((N, 128, C, 4))) * c[:, None, :, None]
    u = d["u"].reshape(N, 128, 8, 16, 4)
    a = 2.0 ** 30 * (1 - 0.1 * rng.random((N, 128, 8, 2, 4))) * np.stack([signs(rng), signs(rng)], axis=2)[:, None, :, :, None]
    u[:, :, :, :2] = a.astype(np.float32).astype(BF)
    w = np.zeros((N, 128, 4, 128, 4), np.float32)
    i = np.arange(128)
    for b in range(4): w[:, i, b, i, b] = -1
    wc, ws = packed(w.reshape(N, 128, 2048).astype(BF), rng)
    return {"x": x.astype(np.float32).reshape(N, 128, 4 * C).astype(BF), "u": u.reshape(N, 128, 512), "v": d["v"], "wc": wc, "ws": ws}
def setup_inputs_cuts(rng):
    d = numbers_of(rng)
    x = d["x"].reshape(N, 8, 16, C, 4)
    u = d["u"].reshape(N, 128, 128, 4)
    x[:, :, 0] = 0
    u[:, :, 1::16] = 0
    u[:, ::16, ::16, 1] = 0
    for h in range(0, 128, 16):
        u[:, h, h + 1, 0] = 1
        u[:, h, h, 1] = 1024
    m = np.arange(1, K)
    end = [C - 1, C - K, C - K + K // 2 - 1]
    for r in range(N):
        way = [m, C - m, np.where(m < K // 2, m, C - K + m), 2 * m, 3 * m, C // K * m, 1 + rng.permutation(C - 1)[:K - 1], np.append([1, C - 1], 2 + rng.permutation(C - 3)[:K - 3])]
        top, last = rng.permutation(8) % 2, rng.permutation(3)
        for g, i in enumerate(rng.permutation(8)):
            s = -1.0 * rng.integers(0, 3, C)
            s[way[i]] = rng.integers(8, 16, K - 1) * 0.125
            s[0] = 4.0 if top[g] else -4.0
            x[r, g, 0, :, 0] = s.astype(np.float32).astype(BF)
            if i < 3 and last[i] < 2:
                x[r, g, 0, end[i], 1] = 64
                if last[i] == 1: x[r, g, 0, end[i] - 1 - int(rng.integers(C - K)), 1] = 128
    return {"x": x.reshape(N, 128, 4 * C), "u": u.reshape(N, 128, 512), "v": d["v"], **weights(rng, [0])}
def setup_inputs_spread(rng):
    d = setup_inputs(rng)
    d["x"] = big(wide(rng, N, 128, 4 * C, cols=6))
    return d
def check_inputs(d):
    b = []
    for k in ("x", "u", "v"):
        a = np.abs(d[k].astype(np.float32))
        if not (np.isfinite(a).all() and ((a == 0) | (a >= 2.0 ** -30) & (a <= 2.0 ** 30)).all()): b.append("a value of " + k)
    if ((d["wc"] & 0x7F) == 0x7F).any(): b.append("a code of wc that is no number")
    z = np.zeros((128, 4, 4), np.float32)
    z[:, 1] = 2.0 ** -30
    z[:, 2] = 2.0 ** 30
    c, s = emit(mx_ref.quantize(z.reshape(128, 16).astype(BF)))
    for r in range(N):
        p = mx_ref.live(d["ws"][r])
        if not ((p == s[0, 0]) | (p >= s[0, 1]) & (p <= s[0, 2])).all(): b.append("a scale of ws")
    return b
def reference(x, u, v, wc, ws):
    qu = [mx_ref.quantize(u[r]) for r in range(N)]
    lay = [pk(wc[r], ws[r]) for r in range(N)]
    now = [x[r] for r in range(N)]
    for t in range(R):
        at, made = [], []
        for r in range(N):
            e, h = runs(mx_ref.matmul(qu[r], mx_ref.quantize(now[r])))
            z = ((gcols(now[r], e).astype(np.float32) + gcols(now[r], h).astype(np.float32)) * np.float32(0.5)).astype(BF)
            at.append(e)
            made.append(mx_ref.quantize(z))
        for r in range(N):
            q = join(pick(made[r], np.arange(C)), pick(made[r ^ STEP[t]], np.arange(C, 2 * C)))
            h = tile([mx_ref.matmul(pick(lay[r], np.arange(128 * b, 128 * b + 128)), q) * np.float32(0.03125) for b in range(4)])
            back = np.argsort(at[r], axis=1, kind="stable")
            s = gcols(h, back[:, ::2]).astype(np.float32) + gcols(h, back[:, 1::2]).astype(np.float32)
            now[r] = (s * np.float32(0.5) + now[r].astype(np.float32)).astype(BF)
    y, ol = np.zeros((N, 128, C), np.float32), np.zeros((N, 8, 2 * C), np.float32)
    oc, osc = np.zeros((N, 128, 4 * C), np.uint8), np.zeros((N, 16, C), np.uint8)
    for r in range(N):
        q = mx_ref.quantize(now[r])
        y[r] = mx_ref.matmul(mx_ref.quantize(v[r]), q)
        ol[r] = at[r]
        oc[r], osc[r] = emit(q)
    return {"y": y, "ol": ol, "oc": oc, "osc": osc}

@@ -1,0 +1,568 @@
+import numpy as np
+from concourse.mybir import dt, AluOpType, AxisListType, ActivationFunctionType
+
+C, K, ROUNDS = 224, 28, 3
+STEP = [3, 1, 2]
+B90 = float(2.0 ** 90)
+LOW = -float(2.0 ** 95)
+BIG = float(2.0 ** 97)
+EW = 464
+CW = 232
+NV = 6
+PASSES = 2
+CYC, WAKE, ROAD = 1.04, 70.0, 3000.0
+
+F32, BF, I32, U16, CODE, U8 = "float32", "bfloat16", "int32", "uint16", "float8_e4m3fn_x4", "uint8"
+_S = {
+    "X0": (896, BF), "X1": (896, BF), "Xh": (896, BF), "qx": (224, CODE), "sx": (224, U8),
+    "ub": (512, BF), "uq": (128, CODE), "us": (128, U8), "up": (512, CODE), "ups": (512, U8),
+    "vb": (512, BF), "vq": (128, CODE), "vs": (128, U8), "wq": (512, CODE), "wsc": (512, U8),
+    "pko": (32, I32), "pk16": (32, U16),
+    "pm": (8, I32), "pf": (16, F32), "i16": (448, BF), "lim": (448, BF), "m01": (64, F32),
+    "r16": (64, F32), "ones": (224, BF), "iot": (CW, F32),
+    "mT": (64, F32), "mTa": (64, F32), "thr": (264, BF), "thra": (272, BF), "cc65": (56, F32), "ccol": (28, F32),
+    "th": (224, F32), "thn": (32, F32), "fl": (223 * NV, BF), "cnt": (223 * NV, BF), "junk": (CW * 8, BF),
+    "acc": (16, F32), "P2": (32, F32), "cand": (32, F32), "candT": (32, F32), "ex": (64, F32), "exT": (64, F32),
+    "t12": (4, F32), "gt": (224, BF), "ge": (224, BF), "ge2": (672, BF), "lim0": (224, BF), "tid1": (224, BF),
+    "lim1": (224, BF), "tid": (CW, BF), "pen": (CW, BF), "q": (CW, F32), "keep": (224, BF), "sv": (CW, F32), "asb": (CW, F32),
+    "M": (224, BF), "inc": (224, BF), "keep2": (224, BF), "SR": (CW, F32), "d2": (CW, BF),
+    "accE": (2, F32), "offE": (2, U16),
+    "aend": (96, F32), "Vr": (64, F32), "endr": (40, F32), "SRe": (32, F32), "d2e": (32, F32),
+    "Vm": (64, F32), "Vx": (64, F32), "D": (256, BF), "fg": (264, F32), "rk": (264, F32), "rk16": (4, U16),
+    "si": (128, I32), "sf": (256, F32), "krow": (64, F32), "k256": (64, F32), "PK": (64, F32),
+    "I": (64, I32), "so": (448, I32), "sg": (128, F32), "PW": (128, F32), "PWx": (128, F32), "oPW": (8, U16),
+    "Vs": (192, F32), "E": (6 * EW, F32), "fill": (896, F32), "EX": (896, F32),
+    "dI": (288, I32), "dF": (256, F32), "F16": (28, U16), "G16": (28, U16),
+    "Af": (1792, BF), "Z": (1792, BF), "Hh": (1792, BF), "Ap": (896, BF), "ss": (896, F32),
+    "tidx": (224, BF), "tid16": (14, U16), "Tt": (320, F32), "RR": (448, F32), "RX": (448, F32), "eI": (288, I32), "pq16": (28, U16),
+    "olr": (448, F32), "yb": (224, F32),
+}
+for _t in range(ROUNDS):
+    _S["qz%d" % _t] = (448, CODE)
+    _S["sz%d" % _t] = (448, U8)
+    _S["lq%d" % _t] = (224, CODE)
+    _S["ls%d" % _t] = (224, U8)
+SCRATCH = {k: ("sbuf", [128, n], d) for k, (n, d) in _S.items()}
+for _b in range(8):
+    SCRATCH["p%d" % _b] = ("psum", [128, 512], F32)
+SEMAPHORES = ["cV", "cS", "cT", "cG", "sent"] + ["arr%d" % t for t in range(ROUNDS)] + ["dm%d" % k for k in range(16)]
+
+
+def rank_program(g, core, T, topo):
+    rank = T.rank_of(core)
+    if rank is None:
+        return
+    A, AF = AluOpType, ActivationFunctionType
+    Q = {"V": g.vector, "S": g.scalar, "T": g.tensor, "G": g, "Y": g.sync}
+    ops = []
+
+    def v(name, a=0, b=None, s=1):
+        return (name, a, SCRATCH[name][1][1] if b is None else b, s)
+
+    def col(name, j):
+        return (name, j, j + 1, 1)
+
+    def ind(w, o):
+        return ("ind", w, o)
+
+    def ap(x):
+        if x[0] == "ind":
+            return ap(x[1]).indirect(ap(x[2]))
+        if x[3] == 1:
+            return T[x[0]][:, x[1]:x[2]]
+        return T[x[0]][:, x[1]:x[2]:x[3]]
+
+    def val(x):
+        return ap(x) if isinstance(x, tuple) else x
+
+    def size(x):
+        return 16 * size(x[2]) if x[0] == "ind" else len(range(x[1], x[2], x[3]))
+
+    def span(out, a, full=False, f=1.0):
+        if out[0] == "ind":
+            return 50 + 3.8 * CYC * size(out)
+        if a[0] == "ind":
+            return 60 + 1.56 * CYC * size(a)
+        if not full and SCRATCH[a[0]][2] == BF and SCRATCH[out[0]][2] in (BF, U16):
+            f = 0.5
+        return max(64, f * size(a)) * CYC
+
+    def add(eng, fn, writes, reads, cost, sem=None, count=16, issue=True, lat=0.0, after=()):
+        w, r = [], []
+        for x in writes:
+            if x[0] == "ind":
+                w.append(x[1])
+                r.append(x[2])
+            else:
+                w.append(x)
+        for x in reads:
+            if isinstance(x, tuple):
+                r += [x[1], x[2]] if x[0] == "ind" else [x]
+        ops.append({"eng": eng, "fn": fn, "w": w, "r": r, "sem": sem, "count": count, "issue": issue, "cost": cost, "lat": lat, "after": list(after)})
+        return len(ops) - 1
+
+    def ts(out, in0, s1, op0, s2=None, op1=None):
+        if op1 is None:
+            return add("V", lambda: g.vector.tensor_scalar(ap(out), ap(in0), val(s1), None, op0), [out], [in0, s1], span(out, in0))
+        return add("V", lambda: g.vector.tensor_scalar(ap(out), ap(in0), val(s1), val(s2), op0, op1), [out], [in0, s1, s2], span(out, in0))
+
+    def tt(out, a, b, op):
+        f = 1.0 if a[0] != "ind" and SCRATCH[a[0]][0] == "psum" else 2.0
+        return add("V", lambda: g.vector.tensor_tensor(ap(out), ap(a), ap(b), op), [out], [a, b], span(out, a, True, f))
+
+    def cp(out, a):
+        return add("V", lambda: g.vector.tensor_copy(ap(out), ap(a)), [out], [a], span(out, a))
+
+    def scan(out, d0, op0, d1, op1, init):
+        return add("V", lambda: g.vector.tensor_tensor_scan(ap(out), ap(d0), ap(d1), val(init), op0, op1), [out], [d0, d1, init],
+                   span(out, d0, SCRATCH[d1[0]][2] != BF))
+
+    def red(out, a, op, neg=False):
+        return add("V", lambda: g.vector.tensor_reduce(ap(out), ap(a), AxisListType.X, op, negate=neg), [out], [a], span(out, a, True))
+
+    def trn(out, a):
+        return add("V", lambda: g.vector.transpose(ap(out), ap(a)), [out], [a], span(out, a))
+
+    def mset(out, c):
+        return add("V", lambda: g.vector.memset(ap(out), c), [out], [], span(out, out))
+
+    def act(out, a, f, bias=0.0, scale=1.0, acc=None):
+        if acc is None:
+            return add("S", lambda: g.scalar.activation(ap(out), ap(a), f, val(bias), val(scale)), [out], [a, bias, scale], span(out, a, True))
+        return add("S", lambda: g.scalar.activation(ap(out), ap(a), f, val(bias), val(scale), accum_out=ap(acc)), [out, acc], [a, bias, scale],
+                   span(out, a, True) + 20)
+
+    def iota(out, pat, base, cm=0):
+        c = 130 + 2 * CYC * size(out)
+        if _S[out[0]][1] == I32:
+            return add("G", lambda: g.iota(ap(out), pat, base, cm), [out], [], c)
+        return add("G", lambda: g.iota(ap(out), pat, base, cm, allow_small_or_imprecise_dtypes=True), [out], [], c)
+
+    def quant(c, s, x):
+        return add("V", lambda: g.vector.quantize_mx(ap(c), ap(s), ap(x)), [c, s], [x], 12 + 0.275 * size(x))
+
+    def mm(bank, n, wc, wsc, xc, xs):
+        return add("T", lambda: g.tensor.matmul_mx(T[bank][:, 0:n], ap(wc), ap(wsc), ap(xc), ap(xs), True, True), [v(bank)], [wc, wsc, xc, xs], 0.9 * (n + 16))
+
+    def chain(l):
+        for a, b in zip(l, l[1:]):
+            ops[b]["after"].append(a)
+
+    ndma = [0]
+
+    def dma(eng, fn, writes, reads):
+        ndma[0] += 1
+        return add(eng, fn, writes, reads, 60.0, sem="dm%d" % (ndma[0] - 1), lat=2000.0)
+
+    def u8(x):
+        return ap(x).bitcast(dt.uint8)
+
+    chain([dma("Y", lambda: g.sync.dma_start(T.ub[:], T.u[:]), [v("ub")], []),
+           dma("Y", lambda: g.sync.dma_start(T.X0[:], T.x[:]), [v("X0")], [])])
+    dma("Y", lambda: g.sync.dma_start(u8(v("wq")), T.wc[:]), [v("wq")], [col("X0", 0)])
+    dma("Y", lambda: g.sync.dma_start(T.wsc[:], T.ws[:]), [v("wsc")], [col("X0", 0)])
+    dma("Y", lambda: g.sync.dma_start(T.vb[:], T.v[:]), [v("vb")], [col("X0", 0)])
+
+    first = [iota(col("pm", 4), [[0, 1]], 0, 1)]
+    for s in range(4):
+        first.append(iota(v("thra", 66 * s + 1, 66 * s + 65), [[1, 2], [2, 32]], -(32 * (s % 2) + s // 2)))
+        iota(col("fg", 66 * s + 65), [[0, 1]], 2 * (32 * (s % 2) + s // 2))
+    first.append(iota(v("pko", 0, 16), [[-1, 2], [16, 8]], 1))
+    first.append(iota(v("pko", 16, 32), [[-16, 2], [32, 4], [0, 2]], 17))
+    chain(first)
+    iota(v("mTa"), [[16, 2], [1, 2], [0, 16]], 0)
+    iota(v("i16"), [[0, 28], [1, 16]], 0)
+    iota(v("iot"), [[1, CW]], 0)
+    iota(v("cc65"), [[0, 2], [16, 28]], -255)
+    iota(v("ccol"), [[0, 2], [16, 14]], -128)
+    iota(v("PW", 57, 64), [[1, 7]], 449 - 255)
+    iota(v("PW", 120, 128), [[1, 8]], 456 - 255)
+    iota(v("Vs"), [[0, 192]], 0)
+    iota(v("SR", C, CW), [[0, 8]], 0)
+    iota(v("d2", C, CW), [[0, 8]], 0)
+    iota(col("keep2", 0), [[0, 1]], 0)
+    iota(col("tid", 0), [[0, 1]], 0)
+    iota(col("endr", 0), [[0, 1]], -1)
+    iota(col("PW", 0), [[0, 1]], -255 * 65536)
+    for k in range(2 * ROUNDS):
+        iota(v("E", EW * k, EW * k + EW), [[0, EW]], -(2 ** 24 - 1))
+
+    cp(v("pk16"), v("pko"))
+    mset(v("ones"), 1.0)
+    mset(v("P2"), BIG)
+    mset(v("thn"), BIG)
+    mset(v("r16"), 1.0)
+    mset(v("r16", 0, 64, 16), 0.0)
+    mset(col("q", 0), -B90)
+    mset(v("pen"), -B90)
+    mset(v("q", C, CW), LOW)
+    mset(v("sv", C, CW), LOW)
+    mset(v("asb", C, CW), LOW)
+    mset(v("tid", C, CW), K * B90)
+    mset(col("lim0", C - 1), (K - 1) * B90)
+    mset(v("thra", 0, 265, 66), 64.0)
+    mset(v("thra", 65, 265, 66), 64.0)
+    ts(col("pm", 0), col("pm", 4), 15, A.bitwise_and)
+    ts(col("pm", 1), col("pm", 4), 17, A.bitwise_and)
+    ts(col("pm", 2), col("pm", 4), 14, A.bitwise_and)
+    cp(v("pf", 0, 3), v("pm", 0, 3))
+    PI = col("pf", 0)
+    ts(col("pf", 3), col("pf", 2), 14.0, A.is_equal, 64.0, A.mult)
+    act(col("pf", 4), PI, AF.Identity, 0.5 * B90, B90)
+    act(col("pf", 5), PI, AF.Identity, 16.5 * B90, B90)
+    act(col("pf", 6), PI, AF.Copy, 0.0, 2.0)
+    act(col("pf", 7), PI, AF.Copy, 0.0, 65536.0)
+    act(col("pf", 8), col("pf", 1), AF.Identity, col("pf", 3))
+    act(col("pf", 9), PI, AF.Copy, 0.0, 4.0)
+    ts(v("mT"), v("mTa"), col("pf", 8), A.not_equal, -0.5, A.add)
+    act(v("mT"), v("mT"), AF.Copy, 0.0, 2 * BIG)
+    ts(v("lim"), v("i16"), PI, A.is_equal, BIG, A.mult)
+    ts(v("m01"), v("i16", 0, 64), PI, A.is_equal)
+    ts(v("thra", 0, 265), v("thra", 0, 265), col("pf", 6), A.is_ge, -0.5, A.add)
+    flips = tt(v("thr"), v("thra", 0, 264), v("thra", 1, 265), A.mult)
+    act(v("thr"), v("thr"), AF.Copy, 0.0, 4.0)
+    mset(v("thr", 0, 264, 66), 0.0)
+    act(v("fg", 65, 264, 66), v("fg", 65, 264, 66), AF.Identity, col("pf", 9))
+    act(v("cc65"), v("cc65"), AF.Identity, col("pf", 7), 65536.0)
+    act(v("ccol"), v("ccol"), AF.Identity, PI)
+    act(v("PW", 57, 64), v("PW", 57, 64), AF.Copy, 0.0, 65536.0)
+    act(v("PW", 120, 128), v("PW", 120, 128), AF.Copy, 0.0, 65536.0)
+
+    chain([flips, quant(v("uq"), v("us"), v("ub"))])
+    for a in (0, 16, 24, 8):
+        o = v("pk16", a, a + 8)
+        c_, s_ = v("up", 16 * a, 16 * a + 128), v("ups", 16 * a, 16 * a + 128)
+        add("V", lambda c_=c_, o=o: g.vector.tensor_copy(ap(c_).bitcast(dt.uint32), ap(v("uq")).bitcast(dt.uint32).indirect(ap(o))), [c_], [v("uq"), o], 260.0)
+        add("S", lambda s_=s_, o=o: g.scalar.activation(ap(s_), ap(v("us")).indirect(ap(o)), AF.Copy), [s_], [v("us"), o], 270.0)
+    quant(v("vq"), v("vs"), v("vb"))
+
+    def ust(k):
+        return v("up", 128 * k, 128 * k + 128), v("ups", 128 * k, 128 * k + 128)
+
+    def wst(b):
+        return v("wq", 128 * b, 128 * b + 128), v("wsc", 128 * b, 128 * b + 128)
+
+    def junk(k, n):
+        return v("junk", CW * k, CW * k + n)
+
+    eng = None
+    for s in STEP:
+        e = set(topo.engines(core, T.cores[rank ^ s]))
+        eng = e if eng is None else eng & e
+    mask = sum(1 << e for e in eng)
+
+    for t in range(ROUNDS):
+        X, Xn = "X%d" % (t % 2), "X%d" % ((t + 1) % 2)
+        qz, sz, lq, ls = "qz%d" % t, "sz%d" % t, "lq%d" % t, "ls%d" % t
+        quant(v("qx"), v("sx"), v(X))
+        for bank, k in (("p0", 0), ("p2", 2), ("p1", 3), ("p3", 2), ("p6", 0), ("p4", 1), ("p5", 1)):
+            mm(bank, C, ust(k)[0], ust(k)[1], v("qx"), v("sx"))
+        trn(v("th"), v("p0", 0, C))
+        for k in range(7):
+            act(junk(k, C - 1), v("p1", 1, C), AF.Sign, col("th", 32 * k), -1.0, col("acc", 2 * k))
+        for k in range(NV, 7):
+            act(junk(7, C - 1), v("p3", 1, C), AF.Sign, col("th", 32 * k + 16), -1.0, col("acc", 2 * k + 1))
+        act(v("thn", 0, 14), v("th", 0, C, 16), AF.Copy)
+        act(v("thn", 16, 30), v("th", 0, C, 16), AF.Copy, 0.0, -1.0)
+        for k in range(NV):
+            fl = v("fl", 223 * k, 223 * k + 223)
+            ts(fl, v("p2", 1, C), col("th", 32 * k + 16), A.is_gt)
+            scan(v("cnt", 223 * k, 223 * k + 223), v("ones", 0, 223), A.mult, fl, A.add, 0.0)
+        ts(v("acc", 1, 2 * NV, 2), v("cnt", 222, 223 * NV, 223), -2.0, A.mult, float(C - 1), A.add)
+        mid = C - 1 - 2 * (K - 1) + 1.5
+        ts(v("P2", 0, 14), v("acc", 0, 14), mid, A.subtract, -1e27, A.mult)
+        ts(v("P2", 16, 30), v("acc", 0, 14), mid, A.subtract, 1e27, A.mult)
+        act(v("asb", 0, C), v("p5", 0, C), AF.Copy)
+        for b in range(4):
+            act(v("Xh", C * b, C * b + C), v(X, b, 4 * C, 4), AF.Copy, 0.0, 0.5)
+        tt(v("cand"), v("thn"), v("P2"), A.max)
+        trn(v("candT"), v("cand"))
+        red(col("t12", 2), v("candT"), A.min)
+        ts(v("ex"), v("mT"), col("t12", 2), A.max)
+        trn(v("exT"), v("ex"))
+        red(col("t12", 1), v("exT", 32, 64), A.min, True)
+        red(col("t12", 0), v("exT", 0, 32), A.min)
+        s_ = v("p0", 1, C)
+        ts(v("gt", 1, C), s_, col("t12", 0), A.is_gt, B90, A.mult)
+        ts(v("ge", 1, C), s_, col("t12", 0), A.is_ge, B90, A.mult)
+        act(v("ge2", C + 1, 2 * C), v("p6", 1, C), AF.Sign, col("t12", 1), -1.0)
+        act(v("ge2", 2 * C + 1, 3 * C), v("ge2", C + 1, 2 * C), AF.Sign, 1.0, -1.0)
+        act(v("ge2", 1, C), v("ge2", 2 * C + 1, 3 * C), AF.Copy, 0.0, B90)
+        scan(v("lim0", C - 2, 0, -1), v("gt", C - 1, 1, -1), A.max, v("gt", C - 1, 1, -1), A.subtract, (K - 1) * B90)
+        scan(v("tid1", 1, C), v("ge", 1, C), A.add, v("lim0", 1, C), A.min, 0.0)
+        ts(v("lim1", 1, C), v("tid1", 1, C), col("tid1", C - 1), A.subtract, (K - 1) * B90, A.add)
+        scan(v("tid", 1, C), v("ge2", 1, C), A.add, v("lim1", 1, C), A.min, 0.0)
+        for k in range(2):
+            act(junk(k, C + 1), v("tid", 0, C + 1), AF.Sign, col("pf", 4 + k), -1.0, col("accE", k))
+        ts(v("offE"), v("accE"), 0.5, A.mult, (C - 1) / 2.0, A.add)
+        scan(v("pen", 1, C), v("tid", 0, C - 1), A.max, v("tid", 1, C), A.subtract, 0.0)
+        scan(v("q", 1, C), v("p4", 0, C - 1), A.max, v("pen", 1, C), A.add, -B90)
+        scan(v("sv", 0, C), v("p4", 0, C), A.max, v("q", 0, C), A.min, -B90)
+        tt(v("keep"), v("p4", 0, C), v("q", 0, C), A.is_le)
+        act(v("M"), v("keep"), AF.Identity, 2.0 ** -8, 1 - 2.0 ** -8)
+        act(v("inc"), v("keep"), AF.Identity, 257.0, -256.0)
+        tt(v("keep2", 1, C), v("p4", 1, C), v("sv", 0, C - 1), A.is_le)
+        scan(v("SR", 0, C), v("ones"), A.add, v("M"), A.mult, 0.0)
+        scan(v("d2", 0, C), v("keep2"), A.mult, v("inc"), A.add, 0.0)
+        oE = v("offE")
+        ende, endp = v("endr", 1, 33), v("endr", 0, 32)
+        act(v("aend", 0, 32), ind(v("asb"), oE), AF.Copy)
+        act(v("aend", 32, 64), ind(v("pen"), oE), AF.Identity, -LOW, -LOW / B90)
+        act(ende, ind(v("iot"), oE), AF.Copy)
+        act(v("SRe"), ind(v("SR"), oE), AF.Identity, -0.44, 256.0)
+        act(v("d2e"), ind(v("d2"), oE), AF.Identity, -1.0)
+        act(v("sf", 0, 32), endp, AF.Identity, 1.0)
+        act(v("sf", 32, 64), endp, AF.Identity, 65280.0, 65279.0)
+        tt(v("Vr", 0, 32), ind(v("q"), oE), v("aend", 0, 32), A.max)
+        tt(v("aend", 64, 96), v("aend", 0, 32), v("aend", 32, 64), A.subtract)
+        tt(v("Vr", 32, 64), ind(v("sv"), oE), v("aend", 64, 96), A.max)
+        tt(v("Vm"), v("Vr"), v("m01"), A.mult)
+        scan(v("Vx"), v("r16"), A.mult, v("Vm"), A.subtract, 0.0)
+        for s in range(4):
+            act(v("D", 64 * s, 64 * s + 64), v("Vr"), AF.Sign, col("Vx", 16 * s + 15), 1.0, col("fg", 66 * s + 64))
+        for s in range(4):
+            act(v("fg", 66 * s, 66 * s + 64), v("D", 64 * s, 64 * s + 64), AF.Abs)
+        scan(v("rk"), v("thr"), A.mult, v("fg"), A.add, 0.0)
+        ts(v("rk16"), v("rk", 65, 264, 66), 0.5, A.mult)
+        cp(v("si", 0, 32), v("SRe"))
+        ts(v("si", 32, 64), v("si", 0, 32), 8, A.arith_shift_right)
+        ts(v("si", 64, 96), v("si", 0, 32), 255, A.bitwise_and)
+        tt(v("krow", 0, 32), ende, v("si", 32, 64), A.subtract)
+        tt(v("sf", 64, 96), ende, v("d2e"), A.subtract)
+        tt(v("sf", 96, 128), v("krow", 0, 32), v("si", 64, 96), A.subtract)
+        tt(v("sf", 160, 192), v("sf", 96, 128), v("sf", 0, 32), A.max)
+        tt(v("sf", 224, 256), v("sf", 32, 64), ende, A.add)
+        tt(v("krow", 32, 64), v("sf", 160, 192), v("sf", 64, 96), A.max)
+        act(v("k256"), v("krow"), AF.Copy, 0.0, 256.0)
+        tt(v("PK", 0, 32), v("k256", 0, 32), v("sf", 224, 256), A.add)
+        tt(v("PK", 32, 64), v("k256", 32, 64), v("sf", 224, 256), A.add)
+        cp(ind(v("I"), v("rk16")), v("PK"))
+        n2 = 2 * K
+        own, nxt = v("I", 0, n2), v("I", 1, n2 + 1)
+
+        def so(k):
+            return v("so", 64 * k, 64 * k + n2)
+        ts(so(0), own, 255, A.bitwise_and)
+        ts(so(1), own, 0xFF00, A.bitwise_and)
+        cp(col("I", n2), col("I", 0))
+        ts(v("sg", 0, n2), so(0), 65536.0, A.mult)
+        ts(v("sg", 64, 64 + n2), so(1), 256.0, A.mult)
+        ts(so(2), own, 8, A.arith_shift_right, 0xFF00, A.bitwise_and)
+        scan(v("PW", 1, n2 + 1), v("ones", 0, n2), A.mult, v("sg", 0, n2), A.add, -255.0 * 65536)
+        ts(so(3), nxt, 16, A.arith_shift_right)
+        ts(so(4), nxt, 0xFFFF, A.bitwise_and)
+        tt(v("PW", 64, 64 + n2), v("PW", 1, n2 + 1), v("sg", 64, 64 + n2), A.subtract)
+        tt(so(5), so(2), so(3), A.add)
+        scan(v("PWx"), v("lim", 0, 128), A.add, v("PW"), A.min, 0.0)
+        ts(v("oPW"), v("PWx", 15, 128, 16), 2.0 ** -16, A.mult, 255.0, A.add)
+        tt(v("Vs", 128, 128 + n2), v("PW", 0, n2), so(4), A.add)
+        tt(so(6), so(5), so(1), A.add)
+        tt(v("Vs", 64, 64 + n2), v("PW", 64, 64 + n2), so(5), A.add)
+        tt(v("Vs", 0, n2), v("PW", 0, n2), so(6), A.add)
+        e1, e2 = 2 * t * EW, (2 * t + 1) * EW
+        cp(ind(v("E", e2, e2 + EW), v("oPW", 0, 4)), v("Vs", 128, 192))
+        cp(ind(v("E", e1, e1 + EW), v("oPW", 4, 8)), v("Vs", 64, 128))
+        cp(ind(v("E", e1, e1 + EW), v("oPW", 0, 4)), v("Vs", 0, 64))
+        scan(v("fill", 448, 896), v("E", e2, e2 + 448), A.max, v("E", e2, e2 + 448), A.max, -BIG)
+        scan(v("EX", 448, 896), v("lim"), A.add, v("fill", 448, 896), A.min, 0.0)
+        scan(v("fill", 0, 448), v("E", e1, e1 + 448), A.max, v("E", e1, e1 + 448), A.max, -BIG)
+        scan(v("EX", 0, 448), v("lim"), A.add, v("fill", 0, 448), A.min, 0.0)
+        tt(v("dI", 0, 56), v("EX", 15, 896, 16), v("cc65"), A.subtract)
+        ts(v("dI", 64, 120), v("dI", 0, 56), 255, A.bitwise_and)
+        ts(v("dI", 128, 184), v("dI", 0, 56), 16, A.arith_shift_right)
+        ts(v("dI", 192, 248), v("dI", 0, 56), 8, A.arith_shift_right, 255, A.bitwise_and)
+        cp(v("dF", 0, 28), v("dI", 92, 120))
+        tt(v("dF", 64, 120), v("dI", 192, 248), v("dI", 128, 184), A.subtract)
+        add("V", lambda: g.vector.reciprocal(ap(v("dF", 32, 60)), ap(v("dF", 0, 28))), [v("dF", 32, 60)], [v("dF", 0, 28)], 410.0)
+        cp(v("F16"), v("dF", 64, 92))
+        tt(v("dF", 128, 156), v("dF", 92, 120), v("dF", 32, 60), A.mult)
+        tt(v("dF", 160, 188), v("dF", 92, 120), v("dI", 64, 92), A.add)
+        ts(v("dI", 256, 284), v("dF", 128, 156), -0.498, A.add)
+        tt(v("dF", 192, 220), v("dI", 256, 284), v("dF", 0, 28), A.mult)
+        tt(v("dF", 224, 252), v("dF", 160, 188), v("dF", 192, 220), A.subtract)
+        cp(v("G16"), v("dF", 224, 252))
+
+        def zhalf(h):
+            ca, cb = [], []
+            for b in range(4):
+                af = v("Af", 896 * h + C * b, 896 * h + C * b + C)
+                ca.append(act(af, ind(v("Xh", C * b, C * b + C), v("F16", 14 * h, 14 * h + 14)), AF.Copy))
+                cb.append(tt(v("Z", 896 * h + b, 896 * h + 896, 4), ind(v("Xh", C * b, C * b + C), v("G16", 14 * h, 14 * h + 14)), af, A.add))
+            chain(ca)
+            chain(cb)
+            return quant(v(qz, C * h, C * h + C), v(sz, C * h, C * h + C), v("Z", 896 * h, 896 * h + 896))
+
+        made = zhalf(1)
+        peer = T.cores[rank ^ STEP[t]]
+        rid, pid, _e = topo.addr(peer)
+        arr = T.sem["arr%d" % t]
+        s1 = add("G", lambda qz=qz, lq=lq, arr=arr, pid=pid, rid=rid:
+                 g.remote_dma(u8(v(lq)), u8(v(qz, C, 2 * C)), arr, T.sem.sent, pid, rid, mask), [], [v(qz, C, 2 * C)], 500.0, sem="remote")
+        s2 = add("G", lambda sz=sz, ls=ls, arr=arr, pid=pid, rid=rid:
+                 g.remote_dma(ap(v(ls)), ap(v(sz, C, 2 * C)), arr, T.sem.sent, pid, rid, mask), [], [v(sz, C, 2 * C)], 500.0, sem="remote", after=[s1])
+        add("R", None, [v(lq), v(ls)], [], ROAD, sem="arr%d" % t, count=2 * len(eng), issue=False, after=[s2])
+        zhalf(0)
+        for b in range(4):
+            mm("p%d" % b, C, wst(b)[0], wst(b)[1], v(qz, 0, C), v(sz, 0, C))
+            lastown = act(v("Hh", 448 * b, 448 * b + C), v("p%d" % b, 0, C), AF.Copy, 0.0, 2.0 ** -6)
+
+        chain([made, scan(v("tidx"), v("lim", 0, C), A.add, v("tid", 0, C), A.min, 0.0)])
+        ts(v("tid16"), v("tidx", 15, C, 16), 1.0 / B90, A.mult)
+        chain([made, tt(v("Tt", 0, 32), ende, endp, A.subtract)])
+        act(v("Tt", 32, 64), v("Tt", 0, 32), AF.Copy)
+        act(v("Tt", 64, 128), ind(v("PW", 0, 64), v("rk16")), AF.Identity, 255.0 * 256, 2.0 ** -8)
+        act(v("Tt", 128, 192), v("krow"), AF.Identity, -(2.0 ** 24), 2.0 ** 17)
+        tt(v("Tt", 192, 256), v("Tt", 128, 192), v("Tt", 0, 64), A.add)
+        tt(v("Tt", 256, 320), v("Tt", 192, 256), v("Tt", 64, 128), A.add)
+        act(v("RR", 0, C), ind(v("Tt", 256, 288), v("tid16")), AF.Copy)
+        act(v("RR", C, 2 * C), ind(v("Tt", 288, 320), v("tid16")), AF.Copy)
+        scan(v("RX"), v("lim"), A.add, v("RR"), A.min, 0.0)
+
+        def eI(k):
+            return v("eI", 32 * k, 32 * k + 28)
+        cp(eI(0), v("RX", 15, 448, 16))
+        ts(eI(1), eI(0), 17, A.arith_shift_right)
+        ts(eI(2), eI(0), 8, A.arith_shift_right, 511, A.bitwise_and)
+        ts(eI(3), eI(0), 255, A.bitwise_and)
+        tt(eI(4), eI(1), v("ccol"), A.subtract)
+        ts(eI(5), eI(4), 0.0, A.max, 256.0, A.mult)
+        tt(eI(6), eI(2), eI(4), A.subtract)
+        tt(eI(7), eI(5), eI(3), A.min)
+        tt(eI(8), eI(6), eI(7), A.add)
+        cp(v("pq16"), eI(8))
+        if t == ROUNDS - 1:
+            act(v("olr"), ind(v("iot"), v("F16")), AF.Copy)
+            dma("Y", lambda: g.sync.dma_start(T.ol[:], T.olr[0:128:16, :]), [], [v("olr")])
+        for b in range(4):
+            mm("p%d" % (4 + b), C, wst(b)[0], wst(b)[1], v(lq), v(ls))
+        z = []
+        for b in range(4):
+            hb, hw = v("Hh", 448 * b + C, 448 * b + 2 * C), v("Hh", 448 * b, 448 * b + 448)
+            if b == 1:
+                z.append(ts(hb, v("p%d" % (4 + b), 0, C), 2.0 ** -6, A.mult))
+            else:
+                z.append(act(hb, v("p%d" % (4 + b), 0, C), AF.Copy, 0.0, 2.0 ** -6))
+            z.append(act(v("Ap", C * b, C * b + C), ind(hw, v("pq16", 0, 14)), AF.Copy))
+            z.append(tt(v("ss", C * b, C * b + C), ind(hw, v("pq16", 14, 28)), v("Ap", C * b, C * b + C), A.add))
+            z.append(tt(v(Xn, b, 4 * C, 4), v("ss", C * b, C * b + C), v(X, b, 4 * C, 4), A.add))
+        chain([z[k] for k in (2, 6, 3, 10, 7, 14, 11, 15)])
+        chain([lastown] + [z[k] for k in (0, 1, 5, 8, 9, 12, 13)])
+
+    quant(v("qx"), v("sx"), v("X%d" % (ROUNDS % 2)))
+    mm("p0", C, v("vq"), v("vs"), v("qx"), v("sx"))
+    dma("Y", lambda: g.sync.dma_start(T.oc[:], u8(v("qx"))), [], [v("qx")])
+    for k in range(4):
+        dma("S" if k < 2 else "Y", lambda k=k: Q["S" if k < 2 else "Y"].dma_start(T.osc[4 * k:4 * k + 4, :], T.sx[32 * k:32 * k + 4, :]), [], [v("sx")])
+    cp(v("yb"), v("p0", 0, C))
+    dma("S", lambda: g.scalar.dma_start(T.y[:], T.yb[:]), [], [v("yb")])
+
+    def cells(x):
+        return np.arange(1) if SCRATCH[x[0]][0] == "psum" else np.arange(x[1], x[2], x[3])
+
+    lastw, readers = {}, {}
+    for i, o in enumerate(ops):
+        deps = set()
+        for x in o["r"] + o["w"]:
+            if x[0] not in lastw:
+                lastw[x[0]] = np.full(SCRATCH[x[0]][1][1], -1)
+                readers[x[0]] = []
+            deps |= set(int(d) for d in np.unique(lastw[x[0]][cells(x)]))
+        for x in o["w"]:
+            cs = set(cells(x).tolist())
+            deps |= set(j for j, c2 in readers[x[0]] if cs & c2)
+            readers[x[0]] = [(j, c2 - cs) for j, c2 in readers[x[0]] if c2 - cs]
+        for x in o["r"]:
+            if SCRATCH[x[0]][0] == "psum":
+                deps |= set(j for j, c2 in readers[x[0]] if ops[j]["eng"] != o["eng"])
+        deps.discard(-1)
+        deps.discard(i)
+        o["deps"] = deps
+        for x in o["w"]:
+            lastw[x[0]][cells(x)] = i
+        for x in o["r"]:
+            readers[x[0]].append((i, set(cells(x).tolist())))
+
+    n = len(ops)
+    pre = [dict([(d, 0.0) for d in o["after"]] + [(d, ops[d]["lat"] + WAKE) for d in o["deps"]]) for o in ops]
+    post = [{} for o in ops]
+    for i in range(n):
+        for d, w in pre[i].items():
+            post[d][i] = w
+
+    def place(before, behind, rank_of, gaps):
+        need = [len(b) for b in before]
+        ready = [i for i in range(n) if not need[i]]
+        at, busy = {}, {}
+        while ready:
+            i = max(ready, key=rank_of)
+            ready.remove(i)
+            c = ops[i]["cost"]
+            s = max([at[d] + ops[d]["cost"] + w for d, w in before[i].items()] + [0.0 if before is pre else ops[i]["lat"]])
+            if gaps:
+                line = busy.setdefault(ops[i]["eng"], [])
+                for a, b in line:
+                    if s + c <= a:
+                        break
+                    s = max(s, b)
+                line.append((s, s + c))
+                line.sort()
+            at[i] = s
+            for j in behind[i]:
+                need[j] -= 1
+                if not need[j]:
+                    ready.append(j)
+        return at
+
+    back = place(post, pre, lambda j: j, False)
+    start, best = None, None
+    for turn in range(PASSES):
+        fwd = place(pre, post, lambda j: (back[j] + ops[j]["cost"], -j), True)
+        end = max(fwd[j] + ops[j]["cost"] + ops[j]["lat"] for j in range(n))
+        if best is None or end < best:
+            start, best = fwd, end
+        back = place(post, pre, lambda j: (fwd[j] + ops[j]["cost"], j), True)
+    order = sorted(range(n), key=lambda j: (start[j], j))
+
+    seq, known, clock, waited = {}, {}, {}, set()
+    for i in order:
+        o = ops[i]
+        o["key"] = o["sem"] if o["sem"] else o["eng"]
+        seq[o["key"]] = seq.get(o["key"], 0) + 1
+        o["seq"] = seq[o["key"]]
+        kn = known.setdefault(o["eng"], {})
+        o["waits"] = []
+        if o["issue"]:
+            for d in sorted(o["deps"], key=lambda j: -start[j]):
+                p = ops[d]
+                if kn.get(p["key"], 0) < p["seq"]:
+                    o["waits"].append(d)
+                    waited.add(d)
+                    for k2, s2 in clock[d].items():
+                        kn[k2] = max(kn.get(k2, 0), s2)
+        clock[i] = dict(kn)
+        clock[i][o["key"]] = o["seq"]
+    total = {}
+    for i in order:
+        o = ops[i]
+        if not o["sem"] and i in waited:
+            total[o["eng"]] = total.get(o["eng"], 0) + 1
+            o["count"] = total[o["eng"]]
+    for i in order:
+        o = ops[i]
+        if not o["issue"]:
+            continue
+        for d in o["waits"]:
+            p = ops[d]
+            Q[o["eng"]].wait_ge(T.sem[p["sem"] if p["sem"] else "c" + p["eng"]], p["count"])
+        ins = o["fn"]()
+        if o["sem"] == "remote":
+            continue
+        if o["sem"]:
+            ins.then_inc(T.sem[o["sem"]], 16)
+        elif i in waited:
+            ins.then_inc(T.sem["c" + o["eng"]], 1)
+    g.wait_ge(T.sem.sent, 2 * len(eng) * ROUNDS)
+    for i in order:
+        o = ops[i]
+        if o["sem"] and o["sem"][:2] == "dm" and i not in waited:
+            g.wait_ge(T.sem[o["sem"]], 16)

@@ -6,11 +6,11 @@ STEP = [3, 1, 2]
 B90 = float(2.0 ** 90)
 LOW = -float(2.0 ** 95)
 BIG = float(2.0 ** 97)
-EW = 464
+EW = 472
 CW = 232
 NV = 6
 PASSES = 2
-CYC, WAKE, ROAD = 1.04, 70.0, 3000.0
+CYC, WAKE, ROAD = 0.9, 220.0, 2500.0
 
 F32, BF, I32, U16, CODE, U8 = "float32", "bfloat16", "int32", "uint16", "float8_e4m3fn_x4", "uint8"
 _S = {
@@ -18,20 +18,21 @@ _S = {
     "ub": (512, BF), "uq": (128, CODE), "us": (128, U8), "up": (512, CODE), "ups": (512, U8),
     "vb": (512, BF), "vq": (128, CODE), "vs": (128, U8), "wq": (512, CODE), "wsc": (512, U8),
     "pko": (32, I32), "pk16": (32, U16),
-    "pm": (8, I32), "pf": (16, F32), "i16": (448, BF), "lim": (448, BF), "m01": (64, F32),
-    "r16": (64, F32), "ones": (224, BF), "iot": (CW, F32),
-    "mT": (64, F32), "mTa": (64, F32), "thr": (264, BF), "thra": (272, BF), "cc65": (56, F32), "ccol": (28, F32),
+    "pm": (8, I32), "pf": (16, F32), "i16": (448, BF), "lim": (448, BF), "mk": (32, F32),
+    "ones": (224, BF), "iot": (CW, F32),
+    "mT": (64, F32), "mTa": (64, F32), "thr": (264, BF), "thra": (272, BF), "cc65": (28, F32), "ccol": (28, F32),
     "th": (224, F32), "thn": (32, F32), "fl": (223 * NV, BF), "cnt": (223 * NV, BF), "junk": (CW * 8, BF),
     "acc": (16, F32), "P2": (32, F32), "cand": (32, F32), "candT": (32, F32), "ex": (64, F32), "exT": (64, F32),
     "t12": (4, F32), "gt": (224, BF), "ge": (224, BF), "ge2": (672, BF), "lim0": (224, BF), "tid1": (224, BF),
-    "lim1": (224, BF), "tid": (CW, BF), "pen": (CW, BF), "q": (CW, F32), "keep": (224, BF), "sv": (CW, F32), "asb": (CW, F32),
+    "lim1": (224, BF), "tid": (CW, BF), "pen": (224, BF), "npen": (224, BF), "q": (224, F32), "top": (CW, F32), "keep": (224, BF),
+    "sv": (CW, F32), "solo": (CW, F32),
     "M": (224, BF), "inc": (224, BF), "keep2": (224, BF), "SR": (CW, F32), "d2": (CW, BF),
     "accE": (2, F32), "offE": (2, U16),
-    "aend": (96, F32), "Vr": (64, F32), "endr": (40, F32), "SRe": (32, F32), "d2e": (32, F32),
-    "Vm": (64, F32), "Vx": (64, F32), "D": (256, BF), "fg": (264, F32), "rk": (264, F32), "rk16": (4, U16),
-    "si": (128, I32), "sf": (256, F32), "krow": (64, F32), "k256": (64, F32), "PK": (64, F32),
-    "I": (64, I32), "so": (448, I32), "sg": (128, F32), "PW": (128, F32), "PWx": (128, F32), "oPW": (8, U16),
-    "Vs": (192, F32), "E": (6 * EW, F32), "fill": (896, F32), "EX": (896, F32),
+    "xm": (96, F32), "nth": (4, F32), "soloE": (32, F32), "Vr": (64, F32), "endr": (40, F32), "SRe": (32, F32), "d2e": (32, F32),
+    "D": (256, BF), "fg": (264, F32), "rk": (264, F32), "rk16": (8, U16),
+    "si": (128, I32), "sf": (256, F32), "krow": (64, F32), "k255": (64, F32), "PK": (64, F32),
+    "I": (64, I32), "so": (448, I32), "sg": (128, F32), "PW": (136, F32), "PWx": (128, F32), "oPW": (8, U16),
+    "Vs": (192, F32), "E": (9 * EW, F32), "fill": (904, F32), "EX": (896, F32),
     "dI": (288, I32), "dF": (256, F32), "F16": (28, U16), "G16": (28, U16),
     "Af": (1792, BF), "Z": (1792, BF), "Hh": (1792, BF), "Ap": (896, BF), "ss": (896, F32),
     "tidx": (224, BF), "tid16": (14, U16), "Tt": (320, F32), "RR": (448, F32), "RX": (448, F32), "eI": (288, I32), "pq16": (28, U16),
@@ -43,7 +44,7 @@ for _t in range(ROUNDS):
     _S["lq%d" % _t] = (224, CODE)
     _S["ls%d" % _t] = (224, U8)
 SCRATCH = {k: ("sbuf", [128, n], d) for k, (n, d) in _S.items()}
-for _b in range(8):
+for _b in (0, 1, 2, 3, 4, 5, 6, 7):
     SCRATCH["p%d" % _b] = ("psum", [128, 512], F32)
 SEMAPHORES = ["cV", "cS", "cT", "cG", "sent"] + ["arr%d" % t for t in range(ROUNDS)] + ["dm%d" % k for k in range(16)]
 
@@ -139,7 +140,7 @@ def rank_program(g, core, T, topo):
         return add("G", lambda: g.iota(ap(out), pat, base, cm, allow_small_or_imprecise_dtypes=True), [out], [], c)
 
     def quant(c, s, x):
-        return add("V", lambda: g.vector.quantize_mx(ap(c), ap(s), ap(x)), [c, s], [x], 12 + 0.275 * size(x))
+        return add("V", lambda: g.vector.quantize_mx(ap(c), ap(s), ap(x)), [c, s], [x], 12 + 0.24 * size(x))
 
     def mm(bank, n, wc, wsc, xc, xs):
         return add("T", lambda: g.tensor.matmul_mx(T[bank][:, 0:n], ap(wc), ap(wsc), ap(xc), ap(xs), True, True), [v(bank)], [wc, wsc, xc, xs], 0.9 * (n + 16))
@@ -164,19 +165,18 @@ def rank_program(g, core, T, topo):
     dma("Y", lambda: g.sync.dma_start(T.vb[:], T.v[:]), [v("vb")], [col("X0", 0)])
 
     first = [iota(col("pm", 4), [[0, 1]], 0, 1)]
+    first.append(iota(v("pko", 0, 16), [[-1, 2], [16, 8]], 1))
+    first.append(iota(v("pko", 16, 32), [[-16, 2], [32, 4], [0, 2]], 17))
     for s in range(4):
         first.append(iota(v("thra", 66 * s + 1, 66 * s + 65), [[1, 2], [2, 32]], -(32 * (s % 2) + s // 2)))
         iota(col("fg", 66 * s + 65), [[0, 1]], 2 * (32 * (s % 2) + s // 2))
-    first.append(iota(v("pko", 0, 16), [[-1, 2], [16, 8]], 1))
-    first.append(iota(v("pko", 16, 32), [[-16, 2], [32, 4], [0, 2]], 17))
     chain(first)
     iota(v("mTa"), [[16, 2], [1, 2], [0, 16]], 0)
     iota(v("i16"), [[0, 28], [1, 16]], 0)
     iota(v("iot"), [[1, CW]], 0)
-    iota(v("cc65"), [[0, 2], [16, 28]], -255)
+    iota(v("cc65"), [[16, 28]], -255)
     iota(v("ccol"), [[0, 2], [16, 14]], -128)
-    iota(v("PW", 57, 64), [[1, 7]], 449 - 255)
-    iota(v("PW", 120, 128), [[1, 8]], 456 - 255)
+    iota(v("PW", 113, 136), [[1, 23]], 449 - 255)
     iota(v("Vs"), [[0, 192]], 0)
     iota(v("SR", C, CW), [[0, 8]], 0)
     iota(v("d2", C, CW), [[0, 8]], 0)
@@ -184,20 +184,18 @@ def rank_program(g, core, T, topo):
     iota(col("tid", 0), [[0, 1]], 0)
     iota(col("endr", 0), [[0, 1]], -1)
     iota(col("PW", 0), [[0, 1]], -255 * 65536)
-    for k in range(2 * ROUNDS):
-        iota(v("E", EW * k, EW * k + EW), [[0, EW]], -(2 ** 24 - 1))
+    for k in range(3 * ROUNDS):
+        iota(v("E", EW * k, EW * k + EW), [[0, EW]], 2 ** 24 - 1)
 
     cp(v("pk16"), v("pko"))
     mset(v("ones"), 1.0)
     mset(v("P2"), BIG)
     mset(v("thn"), BIG)
-    mset(v("r16"), 1.0)
-    mset(v("r16", 0, 64, 16), 0.0)
     mset(col("q", 0), -B90)
-    mset(v("pen"), -B90)
-    mset(v("q", C, CW), LOW)
+    mset(col("pen", 0), -B90)
+    mset(v("top", C, CW), LOW)
     mset(v("sv", C, CW), LOW)
-    mset(v("asb", C, CW), LOW)
+    mset(v("solo", C, CW), LOW)
     mset(v("tid", C, CW), K * B90)
     mset(col("lim0", C - 1), (K - 1) * B90)
     mset(v("thra", 0, 265, 66), 64.0)
@@ -217,23 +215,22 @@ def rank_program(g, core, T, topo):
     ts(v("mT"), v("mTa"), col("pf", 8), A.not_equal, -0.5, A.add)
     act(v("mT"), v("mT"), AF.Copy, 0.0, 2 * BIG)
     ts(v("lim"), v("i16"), PI, A.is_equal, BIG, A.mult)
-    ts(v("m01"), v("i16", 0, 64), PI, A.is_equal)
+    ts(v("mk"), v("i16", 0, 32), PI, A.not_equal, -BIG, A.mult)
     ts(v("thra", 0, 265), v("thra", 0, 265), col("pf", 6), A.is_ge, -0.5, A.add)
-    flips = tt(v("thr"), v("thra", 0, 264), v("thra", 1, 265), A.mult)
+    tt(v("thr"), v("thra", 0, 264), v("thra", 1, 265), A.mult)
     act(v("thr"), v("thr"), AF.Copy, 0.0, 4.0)
     mset(v("thr", 0, 264, 66), 0.0)
     act(v("fg", 65, 264, 66), v("fg", 65, 264, 66), AF.Identity, col("pf", 9))
     act(v("cc65"), v("cc65"), AF.Identity, col("pf", 7), 65536.0)
     act(v("ccol"), v("ccol"), AF.Identity, PI)
-    act(v("PW", 57, 64), v("PW", 57, 64), AF.Copy, 0.0, 65536.0)
-    act(v("PW", 120, 128), v("PW", 120, 128), AF.Copy, 0.0, 65536.0)
+    act(v("PW", 113, 136), v("PW", 113, 136), AF.Copy, 0.0, 65536.0)
 
-    chain([flips, quant(v("uq"), v("us"), v("ub"))])
+    quant(v("uq"), v("us"), v("ub"))
     for a in (0, 16, 24, 8):
         o = v("pk16", a, a + 8)
         c_, s_ = v("up", 16 * a, 16 * a + 128), v("ups", 16 * a, 16 * a + 128)
-        add("V", lambda c_=c_, o=o: g.vector.tensor_copy(ap(c_).bitcast(dt.uint32), ap(v("uq")).bitcast(dt.uint32).indirect(ap(o))), [c_], [v("uq"), o], 260.0)
-        add("S", lambda s_=s_, o=o: g.scalar.activation(ap(s_), ap(v("us")).indirect(ap(o)), AF.Copy), [s_], [v("us"), o], 270.0)
+        add("V", lambda c_=c_, o=o: g.vector.tensor_copy(ap(c_).bitcast(dt.uint32), ap(v("uq")).bitcast(dt.uint32).indirect(ap(o))), [c_], [v("uq"), o], 230.0)
+        add("S", lambda s_=s_, o=o: g.scalar.activation(ap(s_), ap(v("us")).indirect(ap(o)), AF.Copy), [s_], [v("us"), o], 240.0)
     quant(v("vq"), v("vs"), v("vb"))
 
     def ust(k):
@@ -255,7 +252,7 @@ def rank_program(g, core, T, topo):
         X, Xn = "X%d" % (t % 2), "X%d" % ((t + 1) % 2)
         qz, sz, lq, ls = "qz%d" % t, "sz%d" % t, "lq%d" % t, "ls%d" % t
         quant(v("qx"), v("sx"), v(X))
-        for bank, k in (("p0", 0), ("p2", 2), ("p1", 3), ("p3", 2), ("p6", 0), ("p4", 1), ("p5", 1)):
+        for bank, k in (("p0", 0), ("p2", 2), ("p1", 3), ("p3", 2), ("p6", 0), ("p4", 1)):
             mm(bank, C, ust(k)[0], ust(k)[1], v("qx"), v("sx"))
         trn(v("th"), v("p0", 0, C))
         for k in range(7):
@@ -272,7 +269,6 @@ def rank_program(g, core, T, topo):
         mid = C - 1 - 2 * (K - 1) + 1.5
         ts(v("P2", 0, 14), v("acc", 0, 14), mid, A.subtract, -1e27, A.mult)
         ts(v("P2", 16, 30), v("acc", 0, 14), mid, A.subtract, 1e27, A.mult)
-        act(v("asb", 0, C), v("p5", 0, C), AF.Copy)
         for b in range(4):
             act(v("Xh", C * b, C * b + C), v(X, b, 4 * C, 4), AF.Copy, 0.0, 0.5)
         tt(v("cand"), v("thn"), v("P2"), A.max)
@@ -280,14 +276,12 @@ def rank_program(g, core, T, topo):
         red(col("t12", 2), v("candT"), A.min)
         ts(v("ex"), v("mT"), col("t12", 2), A.max)
         trn(v("exT"), v("ex"))
-        red(col("t12", 1), v("exT", 32, 64), A.min, True)
         red(col("t12", 0), v("exT", 0, 32), A.min)
+        red(col("t12", 1), v("exT", 32, 64), A.min, True)
         s_ = v("p0", 1, C)
         ts(v("gt", 1, C), s_, col("t12", 0), A.is_gt, B90, A.mult)
         ts(v("ge", 1, C), s_, col("t12", 0), A.is_ge, B90, A.mult)
-        act(v("ge2", C + 1, 2 * C), v("p6", 1, C), AF.Sign, col("t12", 1), -1.0)
-        act(v("ge2", 2 * C + 1, 3 * C), v("ge2", C + 1, 2 * C), AF.Sign, 1.0, -1.0)
-        act(v("ge2", 1, C), v("ge2", 2 * C + 1, 3 * C), AF.Copy, 0.0, B90)
+        ts(v("ge2", 1, C), s_, col("t12", 1), A.is_ge, B90, A.mult)
         scan(v("lim0", C - 2, 0, -1), v("gt", C - 1, 1, -1), A.max, v("gt", C - 1, 1, -1), A.subtract, (K - 1) * B90)
         scan(v("tid1", 1, C), v("ge", 1, C), A.add, v("lim0", 1, C), A.min, 0.0)
         ts(v("lim1", 1, C), v("tid1", 1, C), col("tid1", C - 1), A.subtract, (K - 1) * B90, A.add)
@@ -295,10 +289,14 @@ def rank_program(g, core, T, topo):
         for k in range(2):
             act(junk(k, C + 1), v("tid", 0, C + 1), AF.Sign, col("pf", 4 + k), -1.0, col("accE", k))
         ts(v("offE"), v("accE"), 0.5, A.mult, (C - 1) / 2.0, A.add)
+        a_ = v("p4", 0, C)
         scan(v("pen", 1, C), v("tid", 0, C - 1), A.max, v("tid", 1, C), A.subtract, 0.0)
+        ts(v("npen"), v("pen"), -1.0, A.mult, -B90, A.add)
         scan(v("q", 1, C), v("p4", 0, C - 1), A.max, v("pen", 1, C), A.add, -B90)
-        scan(v("sv", 0, C), v("p4", 0, C), A.max, v("q", 0, C), A.min, -B90)
-        tt(v("keep"), v("p4", 0, C), v("q", 0, C), A.is_le)
+        scan(v("top", 0, C), v("pen"), A.add, a_, A.max, -B90)
+        scan(v("sv", 0, C), a_, A.max, v("q"), A.min, -B90)
+        tt(v("solo", 0, C), a_, v("npen"), A.add)
+        tt(v("keep"), a_, v("q"), A.is_le)
         act(v("M"), v("keep"), AF.Identity, 2.0 ** -8, 1 - 2.0 ** -8)
         act(v("inc"), v("keep"), AF.Identity, 257.0, -256.0)
         tt(v("keep2", 1, C), v("p4", 1, C), v("sv", 0, C - 1), A.is_le)
@@ -306,81 +304,89 @@ def rank_program(g, core, T, topo):
         scan(v("d2", 0, C), v("keep2"), A.mult, v("inc"), A.add, 0.0)
         oE = v("offE")
         ende, endp = v("endr", 1, 33), v("endr", 0, 32)
-        act(v("aend", 0, 32), ind(v("asb"), oE), AF.Copy)
-        act(v("aend", 32, 64), ind(v("pen"), oE), AF.Identity, -LOW, -LOW / B90)
+        act(v("soloE"), ind(v("solo"), oE), AF.Copy)
+        act(v("Vr", 0, 32), ind(v("top"), oE), AF.Copy)
         act(ende, ind(v("iot"), oE), AF.Copy)
         act(v("SRe"), ind(v("SR"), oE), AF.Identity, -0.44, 256.0)
         act(v("d2e"), ind(v("d2"), oE), AF.Identity, -1.0)
         act(v("sf", 0, 32), endp, AF.Identity, 1.0)
-        act(v("sf", 32, 64), endp, AF.Identity, 65280.0, 65279.0)
-        tt(v("Vr", 0, 32), ind(v("q"), oE), v("aend", 0, 32), A.max)
-        tt(v("aend", 64, 96), v("aend", 0, 32), v("aend", 32, 64), A.subtract)
-        tt(v("Vr", 32, 64), ind(v("sv"), oE), v("aend", 64, 96), A.max)
-        tt(v("Vm"), v("Vr"), v("m01"), A.mult)
-        scan(v("Vx"), v("r16"), A.mult, v("Vm"), A.subtract, 0.0)
+        act(v("sf", 32, 64), endp, AF.Identity, 65281.0, 65280.0)
+        tt(v("Vr", 32, 64), ind(v("sv"), oE), v("soloE"), A.max)
+        tt(v("xm", 0, 32), ind(v("top"), oE), v("mk"), A.add)
+        tt(v("xm", 32, 96, 2), ind(v("sv"), oE), v("mk"), A.add)
+        tt(v("xm", 33, 96, 2), ind(v("solo"), oE), v("mk"), A.add)
+        for s, (a, b) in enumerate(((0, 16), (16, 32), (32, 64), (64, 96))):
+            red(col("nth", s), v("xm", a, b), A.max, True)
         for s in range(4):
-            act(v("D", 64 * s, 64 * s + 64), v("Vr"), AF.Sign, col("Vx", 16 * s + 15), 1.0, col("fg", 66 * s + 64))
-        for s in range(4):
-            act(v("fg", 66 * s, 66 * s + 64), v("D", 64 * s, 64 * s + 64), AF.Abs)
+            act(v("D", 64 * s, 64 * s + 64), v("Vr"), AF.Sign, col("nth", s), 1.0, col("fg", 66 * s + 64))
+            ts(v("fg", 66 * s, 66 * s + 64), v("Vr"), col("nth", s), A.add, 0.0, A.not_equal)
         scan(v("rk"), v("thr"), A.mult, v("fg"), A.add, 0.0)
-        ts(v("rk16"), v("rk", 65, 264, 66), 0.5, A.mult)
+        ts(v("rk16", 0, 4), v("rk", 65, 264, 66), 0.5, A.mult)
         cp(v("si", 0, 32), v("SRe"))
         ts(v("si", 32, 64), v("si", 0, 32), 8, A.arith_shift_right)
         ts(v("si", 64, 96), v("si", 0, 32), 255, A.bitwise_and)
         tt(v("krow", 0, 32), ende, v("si", 32, 64), A.subtract)
         tt(v("sf", 64, 96), ende, v("d2e"), A.subtract)
         tt(v("sf", 96, 128), v("krow", 0, 32), v("si", 64, 96), A.subtract)
-        tt(v("sf", 160, 192), v("sf", 96, 128), v("sf", 0, 32), A.max)
+        tt(v("sf", 160, 192), v("sf", 64, 96), v("sf", 0, 32), A.max)
         tt(v("sf", 224, 256), v("sf", 32, 64), ende, A.add)
-        tt(v("krow", 32, 64), v("sf", 160, 192), v("sf", 64, 96), A.max)
-        act(v("k256"), v("krow"), AF.Copy, 0.0, 256.0)
-        tt(v("PK", 0, 32), v("k256", 0, 32), v("sf", 224, 256), A.add)
-        tt(v("PK", 32, 64), v("k256", 32, 64), v("sf", 224, 256), A.add)
-        cp(ind(v("I"), v("rk16")), v("PK"))
+        tt(v("krow", 32, 64), v("sf", 160, 192), v("sf", 96, 128), A.max)
+        for w in range(2):
+            ts(v("k255", 32 * w, 32 * w + 32), v("krow", 32 * w, 32 * w + 32), 255.0, A.mult)
+            tt(v("PK", 32 * w, 32 * w + 32), v("k255", 32 * w, 32 * w + 32), v("sf", 224, 256), A.add)
+        cp(ind(v("I"), v("rk16", 0, 4)), v("PK"))
         n2 = 2 * K
         own, nxt = v("I", 0, n2), v("I", 1, n2 + 1)
+        P_, W_ = v("PW", 0, 2 * n2, 2), v("PW", 1, 2 * n2, 2)
 
         def so(k):
             return v("so", 64 * k, 64 * k + n2)
         ts(so(0), own, 255, A.bitwise_and)
         ts(so(1), own, 0xFF00, A.bitwise_and)
         cp(col("I", n2), col("I", 0))
-        ts(v("sg", 0, n2), so(0), 65536.0, A.mult)
-        ts(v("sg", 64, 64 + n2), so(1), 256.0, A.mult)
+        ts(v("sg", 0, 2 * n2, 2), so(0), 65536.0, A.mult)
+        ts(v("sg", 1, 2 * n2, 2), so(1), 256.0, A.mult)
         ts(so(2), own, 8, A.arith_shift_right, 0xFF00, A.bitwise_and)
-        scan(v("PW", 1, n2 + 1), v("ones", 0, n2), A.mult, v("sg", 0, n2), A.add, -255.0 * 65536)
+        scan(v("PW", 1, 2 * n2 + 1), v("ones", 0, 2 * n2), A.mult, v("sg", 0, 2 * n2), A.add, -255.0 * 65536)
         ts(so(3), nxt, 16, A.arith_shift_right)
         ts(so(4), nxt, 0xFFFF, A.bitwise_and)
-        tt(v("PW", 64, 64 + n2), v("PW", 1, n2 + 1), v("sg", 64, 64 + n2), A.subtract)
         tt(so(5), so(2), so(3), A.add)
-        scan(v("PWx"), v("lim", 0, 128), A.add, v("PW"), A.min, 0.0)
+        scan(v("PWx", 0, 64), v("lim", 0, 64), A.add, v("PW", 2, 130, 2), A.min, 0.0)
+        scan(v("PWx", 64, 128), v("lim", 0, 64), A.add, v("PW", 1, 129, 2), A.min, 0.0)
         ts(v("oPW"), v("PWx", 15, 128, 16), 2.0 ** -16, A.mult, 255.0, A.add)
-        tt(v("Vs", 128, 128 + n2), v("PW", 0, n2), so(4), A.add)
+        tt(v("Vs", 128, 128 + n2), P_, so(4), A.add)
         tt(so(6), so(5), so(1), A.add)
-        tt(v("Vs", 64, 64 + n2), v("PW", 64, 64 + n2), so(5), A.add)
-        tt(v("Vs", 0, n2), v("PW", 0, n2), so(6), A.add)
-        e1, e2 = 2 * t * EW, (2 * t + 1) * EW
+        tt(v("Vs", 64, 64 + n2), W_, so(5), A.add)
+        tt(v("Vs", 0, n2), P_, so(6), A.add)
+        e0, e1, e2 = 3 * t * EW, (3 * t + 1) * EW, (3 * t + 2) * EW
         cp(ind(v("E", e2, e2 + EW), v("oPW", 0, 4)), v("Vs", 128, 192))
-        cp(ind(v("E", e1, e1 + EW), v("oPW", 4, 8)), v("Vs", 64, 128))
-        cp(ind(v("E", e1, e1 + EW), v("oPW", 0, 4)), v("Vs", 0, 64))
-        scan(v("fill", 448, 896), v("E", e2, e2 + 448), A.max, v("E", e2, e2 + 448), A.max, -BIG)
-        scan(v("EX", 448, 896), v("lim"), A.add, v("fill", 448, 896), A.min, 0.0)
-        scan(v("fill", 0, 448), v("E", e1, e1 + 448), A.max, v("E", e1, e1 + 448), A.max, -BIG)
-        scan(v("EX", 0, 448), v("lim"), A.add, v("fill", 0, 448), A.min, 0.0)
-        tt(v("dI", 0, 56), v("EX", 15, 896, 16), v("cc65"), A.subtract)
-        ts(v("dI", 64, 120), v("dI", 0, 56), 255, A.bitwise_and)
-        ts(v("dI", 128, 184), v("dI", 0, 56), 16, A.arith_shift_right)
-        ts(v("dI", 192, 248), v("dI", 0, 56), 8, A.arith_shift_right, 255, A.bitwise_and)
-        cp(v("dF", 0, 28), v("dI", 92, 120))
-        tt(v("dF", 64, 120), v("dI", 192, 248), v("dI", 128, 184), A.subtract)
-        add("V", lambda: g.vector.reciprocal(ap(v("dF", 32, 60)), ap(v("dF", 0, 28))), [v("dF", 32, 60)], [v("dF", 0, 28)], 410.0)
-        cp(v("F16"), v("dF", 64, 92))
-        tt(v("dF", 128, 156), v("dF", 92, 120), v("dF", 32, 60), A.mult)
-        tt(v("dF", 160, 188), v("dF", 92, 120), v("dI", 64, 92), A.add)
-        ts(v("dI", 256, 284), v("dF", 128, 156), -0.498, A.add)
-        tt(v("dF", 192, 220), v("dI", 256, 284), v("dF", 0, 28), A.mult)
-        tt(v("dF", 224, 252), v("dF", 160, 188), v("dF", 192, 220), A.subtract)
-        cp(v("G16"), v("dF", 224, 252))
+        cp(ind(v("E", e1, e1 + EW), v("oPW", 0, 4)), v("Vs", 64, 128))
+        cp(ind(v("E", e0, e0 + EW), v("oPW", 4, 8)), v("Vs", 0, 64))
+        scan(v("fill", 903, 455, -1), v("E", e2 + 448, e2, -1), A.min, v("E", e2 + 448, e2, -1), A.min, BIG)
+        scan(v("EX", 448, 896), v("lim"), A.add, v("fill", 456, 904), A.min, 0.0)
+        scan(v("fill", 455, 7, -1), v("E", e1 + 448, e1, -1), A.min, v("E", e0 + 448, e0, -1), A.min, BIG)
+        scan(v("EX", 0, 448), v("lim"), A.add, v("fill", 8, 456), A.min, 0.0)
+
+        def dI(k):
+            return v("dI", 32 * k, 32 * k + 28)
+
+        def dF(k):
+            return v("dF", 32 * k, 32 * k + 28)
+        for r in (1, 0):
+            tt(dI(4 * r), v("EX", 448 * r + 15, 448 * r + 448, 16), v("cc65"), A.subtract)
+            ts(dI(4 * r + 1), dI(4 * r), 255, A.bitwise_and)
+            ts(dI(4 * r + 2), dI(4 * r), 8, A.arith_shift_right, 255, A.bitwise_and)
+            ts(dI(4 * r + 3), dI(4 * r), 16, A.arith_shift_right)
+            tt(dF(r), dI(4 * r + 2), dI(4 * r + 3), A.subtract)
+        cp(v("F16"), dF(0))
+        tt(dF(2), dI(5), dI(6), A.add)
+        add("V", lambda: g.vector.reciprocal(ap(dF(3)), ap(dF(2))), [dF(3)], [dF(2)], 360.0)
+        tt(dF(4), dF(1), dF(3), A.mult)
+        tt(dF(5), dF(1), dI(1), A.add)
+        ts(dI(8), dF(4), -0.498, A.add)
+        tt(dF(6), dI(8), dF(2), A.mult)
+        tt(dF(7), dF(5), dF(6), A.subtract)
+        cp(v("G16"), dF(7))
 
         def zhalf(h):
             ca, cb = [], []
@@ -397,20 +403,22 @@ def rank_program(g, core, T, topo):
         rid, pid, _e = topo.addr(peer)
         arr = T.sem["arr%d" % t]
         s1 = add("G", lambda qz=qz, lq=lq, arr=arr, pid=pid, rid=rid:
-                 g.remote_dma(u8(v(lq)), u8(v(qz, C, 2 * C)), arr, T.sem.sent, pid, rid, mask), [], [v(qz, C, 2 * C)], 500.0, sem="remote")
+                 g.remote_dma(u8(v(lq)), u8(v(qz, C, 2 * C)), arr, T.sem.sent, pid, rid, mask), [], [v(qz, C, 2 * C)], 300.0, sem="remote")
         s2 = add("G", lambda sz=sz, ls=ls, arr=arr, pid=pid, rid=rid:
-                 g.remote_dma(ap(v(ls)), ap(v(sz, C, 2 * C)), arr, T.sem.sent, pid, rid, mask), [], [v(sz, C, 2 * C)], 500.0, sem="remote", after=[s1])
+                 g.remote_dma(ap(v(ls)), ap(v(sz, C, 2 * C)), arr, T.sem.sent, pid, rid, mask), [], [v(sz, C, 2 * C)], 300.0, sem="remote", after=[s1])
         add("R", None, [v(lq), v(ls)], [], ROAD, sem="arr%d" % t, count=2 * len(eng), issue=False, after=[s2])
         zhalf(0)
+        mms = []
         for b in range(4):
-            mm("p%d" % b, C, wst(b)[0], wst(b)[1], v(qz, 0, C), v(sz, 0, C))
+            mms.append(mm("p%d" % b, C, wst(b)[0], wst(b)[1], v(qz, 0, C), v(sz, 0, C)))
             lastown = act(v("Hh", 448 * b, 448 * b + C), v("p%d" % b, 0, C), AF.Copy, 0.0, 2.0 ** -6)
 
-        chain([made, scan(v("tidx"), v("lim", 0, C), A.add, v("tid", 0, C), A.min, 0.0)])
+        scan(v("tidx"), v("lim", 0, C), A.add, v("tid", 0, C), A.min, 0.0)
         ts(v("tid16"), v("tidx", 15, C, 16), 1.0 / B90, A.mult)
-        chain([made, tt(v("Tt", 0, 32), ende, endp, A.subtract)])
+        cp(v("rk16", 4, 8), v("rk", 65, 264, 66))
+        tt(v("Tt", 0, 32), ende, endp, A.subtract)
         act(v("Tt", 32, 64), v("Tt", 0, 32), AF.Copy)
-        act(v("Tt", 64, 128), ind(v("PW", 0, 64), v("rk16")), AF.Identity, 255.0 * 256, 2.0 ** -8)
+        act(v("Tt", 64, 128), ind(v("PW"), v("rk16", 4, 8)), AF.Identity, 255.0 * 256, 2.0 ** -8)
         act(v("Tt", 128, 192), v("krow"), AF.Identity, -(2.0 ** 24), 2.0 ** 17)
         tt(v("Tt", 192, 256), v("Tt", 128, 192), v("Tt", 0, 64), A.add)
         tt(v("Tt", 256, 320), v("Tt", 192, 256), v("Tt", 64, 128), A.add)
@@ -434,7 +442,8 @@ def rank_program(g, core, T, topo):
             act(v("olr"), ind(v("iot"), v("F16")), AF.Copy)
             dma("Y", lambda: g.sync.dma_start(T.ol[:], T.olr[0:128:16, :]), [], [v("olr")])
         for b in range(4):
-            mm("p%d" % (4 + b), C, wst(b)[0], wst(b)[1], v(lq), v(ls))
+            mms.append(mm("p%d" % (4 + b), C, wst(b)[0], wst(b)[1], v(lq), v(ls)))
+        chain(mms)
         z = []
         for b in range(4):
             hb, hw = v("Hh", 448 * b + C, 448 * b + 2 * C), v("Hh", 448 * b, 448 * b + 448)
@@ -446,7 +455,7 @@ def rank_program(g, core, T, topo):
             z.append(tt(v("ss", C * b, C * b + C), ind(hw, v("pq16", 14, 28)), v("Ap", C * b, C * b + C), A.add))
             z.append(tt(v(Xn, b, 4 * C, 4), v("ss", C * b, C * b + C), v(X, b, 4 * C, 4), A.add))
         chain([z[k] for k in (2, 6, 3, 10, 7, 14, 11, 15)])
-        chain([lastown] + [z[k] for k in (0, 1, 5, 8, 9, 12, 13)])
+        chain([lastown] + [z[k] for k in (0, 8, 1, 5, 12, 9, 13)])
 
     quant(v("qx"), v("sx"), v("X%d" % (ROUNDS % 2)))
     mm("p0", C, v("vq"), v("vs"), v("qx"), v("sx"))

import numpy as np
from concourse.mybir import dt, AluOpType, AxisListType, ActivationFunctionType

C, K, ROUNDS = 224, 28, 3
STEP = [3, 1, 2]
B90 = float(2.0 ** 90)
LOW = -float(2.0 ** 95)
BIG = float(2.0 ** 97)
EW = 472
CW = 232
NV = 6
PASSES = 2
CYC, WAKE, ROAD = 0.9, 220.0, 2500.0

F32, BF, I32, U16, CODE, U8 = "float32", "bfloat16", "int32", "uint16", "float8_e4m3fn_x4", "uint8"
_S = {
    "X0": (896, BF), "X1": (896, BF), "Xh": (896, BF), "qx": (224, CODE), "sx": (224, U8),
    "ub": (512, BF), "uq": (128, CODE), "us": (128, U8), "up": (512, CODE), "ups": (512, U8),
    "vb": (512, BF), "vq": (128, CODE), "vs": (128, U8), "wq": (512, CODE), "wsc": (512, U8),
    "pko": (32, I32), "pk16": (32, U16),
    "pm": (8, I32), "pf": (16, F32), "i16": (448, BF), "lim": (448, BF), "mk": (32, F32),
    "ones": (224, BF), "iot": (CW, F32),
    "mT": (64, F32), "mTa": (64, F32), "thr": (264, BF), "thra": (272, BF), "cc65": (28, F32), "ccol": (28, F32),
    "th": (224, F32), "thn": (32, F32), "fl": (223 * NV, BF), "cnt": (223 * NV, BF), "junk": (CW * 8, BF),
    "acc": (16, F32), "P2": (32, F32), "cand": (32, F32), "candT": (32, F32), "ex": (64, F32), "exT": (64, F32),
    "t12": (4, F32), "gt": (224, BF), "ge": (224, BF), "ge2": (672, BF), "lim0": (224, BF), "tid1": (224, BF),
    "lim1": (224, BF), "tid": (CW, BF), "pen": (224, BF), "npen": (224, BF), "q": (224, F32), "top": (CW, F32), "keep": (224, BF),
    "sv": (CW, F32), "solo": (CW, F32),
    "M": (224, BF), "inc": (224, BF), "keep2": (224, BF), "SR": (CW, F32), "d2": (CW, BF),
    "accE": (2, F32), "offE": (2, U16),
    "xm": (96, F32), "nth": (4, F32), "soloE": (32, F32), "Vr": (64, F32), "endr": (40, F32), "SRe": (32, F32), "d2e": (32, F32),
    "D": (256, BF), "fg": (264, F32), "rk": (264, F32), "rk16": (8, U16),
    "si": (128, I32), "sf": (256, F32), "krow": (64, F32), "k255": (64, F32), "PK": (64, F32),
    "I": (64, I32), "so": (448, I32), "sg": (128, F32), "PW": (136, F32), "PWx": (128, F32), "oPW": (8, U16),
    "Vs": (192, F32), "E": (9 * EW, F32), "fill": (904, F32), "EX": (896, F32),
    "dI": (288, I32), "dF": (256, F32), "F16": (28, U16), "G16": (28, U16),
    "Af": (1792, BF), "Z": (1792, BF), "Hh": (1792, BF), "Ap": (896, BF), "ss": (896, F32),
    "tidx": (224, BF), "tid16": (14, U16), "Tt": (320, F32), "RR": (448, F32), "RX": (448, F32), "eI": (288, I32), "pq16": (28, U16),
    "olr": (448, F32), "yb": (224, F32),
}
for _t in range(ROUNDS):
    _S["qz%d" % _t] = (448, CODE)
    _S["sz%d" % _t] = (448, U8)
    _S["lq%d" % _t] = (224, CODE)
    _S["ls%d" % _t] = (224, U8)
SCRATCH = {k: ("sbuf", [128, n], d) for k, (n, d) in _S.items()}
for _b in (0, 1, 2, 3, 4, 5, 6, 7):
    SCRATCH["p%d" % _b] = ("psum", [128, 512], F32)
SEMAPHORES = ["cV", "cS", "cT", "cG", "sent"] + ["arr%d" % t for t in range(ROUNDS)] + ["dm%d" % k for k in range(16)]


def rank_program(g, core, T, topo):
    rank = T.rank_of(core)
    if rank is None:
        return
    A, AF = AluOpType, ActivationFunctionType
    Q = {"V": g.vector, "S": g.scalar, "T": g.tensor, "G": g, "Y": g.sync}
    ops = []

    def v(name, a=0, b=None, s=1):
        return (name, a, SCRATCH[name][1][1] if b is None else b, s)

    def col(name, j):
        return (name, j, j + 1, 1)

    def ind(w, o):
        return ("ind", w, o)

    def ap(x):
        if x[0] == "ind":
            return ap(x[1]).indirect(ap(x[2]))
        if x[3] == 1:
            return T[x[0]][:, x[1]:x[2]]
        return T[x[0]][:, x[1]:x[2]:x[3]]

    def val(x):
        return ap(x) if isinstance(x, tuple) else x

    def size(x):
        return 16 * size(x[2]) if x[0] == "ind" else len(range(x[1], x[2], x[3]))

    def span(out, a, full=False, f=1.0):
        if out[0] == "ind":
            return 50 + 3.8 * CYC * size(out)
        if a[0] == "ind":
            return 60 + 1.56 * CYC * size(a)
        if not full and SCRATCH[a[0]][2] == BF and SCRATCH[out[0]][2] in (BF, U16):
            f = 0.5
        return max(64, f * size(a)) * CYC

    def add(eng, fn, writes, reads, cost, sem=None, count=16, issue=True, lat=0.0, after=()):
        w, r = [], []
        for x in writes:
            if x[0] == "ind":
                w.append(x[1])
                r.append(x[2])
            else:
                w.append(x)
        for x in reads:
            if isinstance(x, tuple):
                r += [x[1], x[2]] if x[0] == "ind" else [x]
        ops.append({"eng": eng, "fn": fn, "w": w, "r": r, "sem": sem, "count": count, "issue": issue, "cost": cost, "lat": lat, "after": list(after)})
        return len(ops) - 1

    def ts(out, in0, s1, op0, s2=None, op1=None):
        if op1 is None:
            return add("V", lambda: g.vector.tensor_scalar(ap(out), ap(in0), val(s1), None, op0), [out], [in0, s1], span(out, in0))
        return add("V", lambda: g.vector.tensor_scalar(ap(out), ap(in0), val(s1), val(s2), op0, op1), [out], [in0, s1, s2], span(out, in0))

    def tt(out, a, b, op):
        f = 1.0 if a[0] != "ind" and SCRATCH[a[0]][0] == "psum" else 2.0
        return add("V", lambda: g.vector.tensor_tensor(ap(out), ap(a), ap(b), op), [out], [a, b], span(out, a, True, f))

    def cp(out, a):
        return add("V", lambda: g.vector.tensor_copy(ap(out), ap(a)), [out], [a], span(out, a))

    def scan(out, d0, op0, d1, op1, init):
        return add("V", lambda: g.vector.tensor_tensor_scan(ap(out), ap(d0), ap(d1), val(init), op0, op1), [out], [d0, d1, init],
                   span(out, d0, SCRATCH[d1[0]][2] != BF))

    def red(out, a, op, neg=False):
        return add("V", lambda: g.vector.tensor_reduce(ap(out), ap(a), AxisListType.X, op, negate=neg), [out], [a], span(out, a, True))

    def trn(out, a):
        return add("V", lambda: g.vector.transpose(ap(out), ap(a)), [out], [a], span(out, a))

    def mset(out, c):
        return add("V", lambda: g.vector.memset(ap(out), c), [out], [], span(out, out))

    def act(out, a, f, bias=0.0, scale=1.0, acc=None):
        if acc is None:
            return add("S", lambda: g.scalar.activation(ap(out), ap(a), f, val(bias), val(scale)), [out], [a, bias, scale], span(out, a, True))
        return add("S", lambda: g.scalar.activation(ap(out), ap(a), f, val(bias), val(scale), accum_out=ap(acc)), [out, acc], [a, bias, scale],
                   span(out, a, True) + 20)

    def iota(out, pat, base, cm=0):
        c = 130 + 2 * CYC * size(out)
        if _S[out[0]][1] == I32:
            return add("G", lambda: g.iota(ap(out), pat, base, cm), [out], [], c)
        return add("G", lambda: g.iota(ap(out), pat, base, cm, allow_small_or_imprecise_dtypes=True), [out], [], c)

    def quant(c, s, x):
        return add("V", lambda: g.vector.quantize_mx(ap(c), ap(s), ap(x)), [c, s], [x], 12 + 0.24 * size(x))

    def mm(bank, n, wc, wsc, xc, xs):
        return add("T", lambda: g.tensor.matmul_mx(T[bank][:, 0:n], ap(wc), ap(wsc), ap(xc), ap(xs), True, True), [v(bank)], [wc, wsc, xc, xs], 0.9 * (n + 16))

    def chain(l):
        for a, b in zip(l, l[1:]):
            ops[b]["after"].append(a)

    ndma = [0]

    def dma(eng, fn, writes, reads):
        ndma[0] += 1
        return add(eng, fn, writes, reads, 60.0, sem="dm%d" % (ndma[0] - 1), lat=2000.0)

    def u8(x):
        return ap(x).bitcast(dt.uint8)

    chain([dma("Y", lambda: g.sync.dma_start(T.ub[:], T.u[:]), [v("ub")], []),
           dma("Y", lambda: g.sync.dma_start(T.X0[:], T.x[:]), [v("X0")], [])])
    dma("Y", lambda: g.sync.dma_start(u8(v("wq")), T.wc[:]), [v("wq")], [col("X0", 0)])
    dma("Y", lambda: g.sync.dma_start(T.wsc[:], T.ws[:]), [v("wsc")], [col("X0", 0)])
    dma("Y", lambda: g.sync.dma_start(T.vb[:], T.v[:]), [v("vb")], [col("X0", 0)])

    first = [iota(col("pm", 4), [[0, 1]], 0, 1)]
    first.append(iota(v("pko", 0, 16), [[-1, 2], [16, 8]], 1))
    first.append(iota(v("pko", 16, 32), [[-16, 2], [32, 4], [0, 2]], 17))
    for s in range(4):
        first.append(iota(v("thra", 66 * s + 1, 66 * s + 65), [[1, 2], [2, 32]], -(32 * (s % 2) + s // 2)))
        iota(col("fg", 66 * s + 65), [[0, 1]], 2 * (32 * (s % 2) + s // 2))
    chain(first)
    iota(v("mTa"), [[16, 2], [1, 2], [0, 16]], 0)
    iota(v("i16"), [[0, 28], [1, 16]], 0)
    iota(v("iot"), [[1, CW]], 0)
    iota(v("cc65"), [[16, 28]], -255)
    iota(v("ccol"), [[0, 2], [16, 14]], -128)
    iota(v("PW", 113, 136), [[1, 23]], 449 - 255)
    iota(v("Vs"), [[0, 192]], 0)
    iota(v("SR", C, CW), [[0, 8]], 0)
    iota(v("d2", C, CW), [[0, 8]], 0)
    iota(col("keep2", 0), [[0, 1]], 0)
    iota(col("tid", 0), [[0, 1]], 0)
    iota(col("endr", 0), [[0, 1]], -1)
    iota(col("PW", 0), [[0, 1]], -255 * 65536)
    for k in range(3 * ROUNDS):
        iota(v("E", EW * k, EW * k + EW), [[0, EW]], 2 ** 24 - 1)

    cp(v("pk16"), v("pko"))
    mset(v("ones"), 1.0)
    mset(v("P2"), BIG)
    mset(v("thn"), BIG)
    mset(col("q", 0), -B90)
    mset(col("pen", 0), -B90)
    mset(v("top", C, CW), LOW)
    mset(v("sv", C, CW), LOW)
    mset(v("solo", C, CW), LOW)
    mset(v("tid", C, CW), K * B90)
    mset(col("lim0", C - 1), (K - 1) * B90)
    mset(v("thra", 0, 265, 66), 64.0)
    mset(v("thra", 65, 265, 66), 64.0)
    ts(col("pm", 0), col("pm", 4), 15, A.bitwise_and)
    ts(col("pm", 1), col("pm", 4), 17, A.bitwise_and)
    ts(col("pm", 2), col("pm", 4), 14, A.bitwise_and)
    cp(v("pf", 0, 3), v("pm", 0, 3))
    PI = col("pf", 0)
    ts(col("pf", 3), col("pf", 2), 14.0, A.is_equal, 64.0, A.mult)
    act(col("pf", 4), PI, AF.Identity, 0.5 * B90, B90)
    act(col("pf", 5), PI, AF.Identity, 16.5 * B90, B90)
    act(col("pf", 6), PI, AF.Copy, 0.0, 2.0)
    act(col("pf", 7), PI, AF.Copy, 0.0, 65536.0)
    act(col("pf", 8), col("pf", 1), AF.Identity, col("pf", 3))
    act(col("pf", 9), PI, AF.Copy, 0.0, 4.0)
    ts(v("mT"), v("mTa"), col("pf", 8), A.not_equal, -0.5, A.add)
    act(v("mT"), v("mT"), AF.Copy, 0.0, 2 * BIG)
    ts(v("lim"), v("i16"), PI, A.is_equal, BIG, A.mult)
    ts(v("mk"), v("i16", 0, 32), PI, A.not_equal, -BIG, A.mult)
    ts(v("thra", 0, 265), v("thra", 0, 265), col("pf", 6), A.is_ge, -0.5, A.add)
    tt(v("thr"), v("thra", 0, 264), v("thra", 1, 265), A.mult)
    act(v("thr"), v("thr"), AF.Copy, 0.0, 4.0)
    mset(v("thr", 0, 264, 66), 0.0)
    act(v("fg", 65, 264, 66), v("fg", 65, 264, 66), AF.Identity, col("pf", 9))
    act(v("cc65"), v("cc65"), AF.Identity, col("pf", 7), 65536.0)
    act(v("ccol"), v("ccol"), AF.Identity, PI)
    act(v("PW", 113, 136), v("PW", 113, 136), AF.Copy, 0.0, 65536.0)

    quant(v("uq"), v("us"), v("ub"))
    for a in (0, 16, 24, 8):
        o = v("pk16", a, a + 8)
        c_, s_ = v("up", 16 * a, 16 * a + 128), v("ups", 16 * a, 16 * a + 128)
        add("V", lambda c_=c_, o=o: g.vector.tensor_copy(ap(c_).bitcast(dt.uint32), ap(v("uq")).bitcast(dt.uint32).indirect(ap(o))), [c_], [v("uq"), o], 230.0)
        add("S", lambda s_=s_, o=o: g.scalar.activation(ap(s_), ap(v("us")).indirect(ap(o)), AF.Copy), [s_], [v("us"), o], 240.0)
    quant(v("vq"), v("vs"), v("vb"))

    def ust(k):
        return v("up", 128 * k, 128 * k + 128), v("ups", 128 * k, 128 * k + 128)

    def wst(b):
        return v("wq", 128 * b, 128 * b + 128), v("wsc", 128 * b, 128 * b + 128)

    def junk(k, n):
        return v("junk", CW * k, CW * k + n)

    eng = None
    for s in STEP:
        e = set(topo.engines(core, T.cores[rank ^ s]))
        eng = e if eng is None else eng & e
    mask = sum(1 << e for e in eng)

    for t in range(ROUNDS):
        X, Xn = "X%d" % (t % 2), "X%d" % ((t + 1) % 2)
        qz, sz, lq, ls = "qz%d" % t, "sz%d" % t, "lq%d" % t, "ls%d" % t
        quant(v("qx"), v("sx"), v(X))
        for bank, k in (("p0", 0), ("p2", 2), ("p1", 3), ("p3", 2), ("p6", 0), ("p4", 1)):
            mm(bank, C, ust(k)[0], ust(k)[1], v("qx"), v("sx"))
        trn(v("th"), v("p0", 0, C))
        for k in range(7):
            act(junk(k, C - 1), v("p1", 1, C), AF.Sign, col("th", 32 * k), -1.0, col("acc", 2 * k))
        for k in range(NV, 7):
            act(junk(7, C - 1), v("p3", 1, C), AF.Sign, col("th", 32 * k + 16), -1.0, col("acc", 2 * k + 1))
        act(v("thn", 0, 14), v("th", 0, C, 16), AF.Copy)
        act(v("thn", 16, 30), v("th", 0, C, 16), AF.Copy, 0.0, -1.0)
        for k in range(NV):
            fl = v("fl", 223 * k, 223 * k + 223)
            ts(fl, v("p2", 1, C), col("th", 32 * k + 16), A.is_gt)
            scan(v("cnt", 223 * k, 223 * k + 223), v("ones", 0, 223), A.mult, fl, A.add, 0.0)
        ts(v("acc", 1, 2 * NV, 2), v("cnt", 222, 223 * NV, 223), -2.0, A.mult, float(C - 1), A.add)
        mid = C - 1 - 2 * (K - 1) + 1.5
        ts(v("P2", 0, 14), v("acc", 0, 14), mid, A.subtract, -1e27, A.mult)
        ts(v("P2", 16, 30), v("acc", 0, 14), mid, A.subtract, 1e27, A.mult)
        for b in range(4):
            act(v("Xh", C * b, C * b + C), v(X, b, 4 * C, 4), AF.Copy, 0.0, 0.5)
        tt(v("cand"), v("thn"), v("P2"), A.max)
        trn(v("candT"), v("cand"))
        red(col("t12", 2), v("candT"), A.min)
        ts(v("ex"), v("mT"), col("t12", 2), A.max)
        trn(v("exT"), v("ex"))
        red(col("t12", 0), v("exT", 0, 32), A.min)
        red(col("t12", 1), v("exT", 32, 64), A.min, True)
        s_ = v("p0", 1, C)
        ts(v("gt", 1, C), s_, col("t12", 0), A.is_gt, B90, A.mult)
        ts(v("ge", 1, C), s_, col("t12", 0), A.is_ge, B90, A.mult)
        ts(v("ge2", 1, C), s_, col("t12", 1), A.is_ge, B90, A.mult)
        scan(v("lim0", C - 2, 0, -1), v("gt", C - 1, 1, -1), A.max, v("gt", C - 1, 1, -1), A.subtract, (K - 1) * B90)
        scan(v("tid1", 1, C), v("ge", 1, C), A.add, v("lim0", 1, C), A.min, 0.0)
        ts(v("lim1", 1, C), v("tid1", 1, C), col("tid1", C - 1), A.subtract, (K - 1) * B90, A.add)
        scan(v("tid", 1, C), v("ge2", 1, C), A.add, v("lim1", 1, C), A.min, 0.0)
        for k in range(2):
            act(junk(k, C + 1), v("tid", 0, C + 1), AF.Sign, col("pf", 4 + k), -1.0, col("accE", k))
        ts(v("offE"), v("accE"), 0.5, A.mult, (C - 1) / 2.0, A.add)
        a_ = v("p4", 0, C)
        scan(v("pen", 1, C), v("tid", 0, C - 1), A.max, v("tid", 1, C), A.subtract, 0.0)
        ts(v("npen"), v("pen"), -1.0, A.mult, -B90, A.add)
        scan(v("q", 1, C), v("p4", 0, C - 1), A.max, v("pen", 1, C), A.add, -B90)
        scan(v("top", 0, C), v("pen"), A.add, a_, A.max, -B90)
        scan(v("sv", 0, C), a_, A.max, v("q"), A.min, -B90)
        tt(v("solo", 0, C), a_, v("npen"), A.add)
        tt(v("keep"), a_, v("q"), A.is_le)
        act(v("M"), v("keep"), AF.Identity, 2.0 ** -8, 1 - 2.0 ** -8)
        act(v("inc"), v("keep"), AF.Identity, 257.0, -256.0)
        tt(v("keep2", 1, C), v("p4", 1, C), v("sv", 0, C - 1), A.is_le)
        scan(v("SR", 0, C), v("ones"), A.add, v("M"), A.mult, 0.0)
        scan(v("d2", 0, C), v("keep2"), A.mult, v("inc"), A.add, 0.0)
        oE = v("offE")
        ende, endp = v("endr", 1, 33), v("endr", 0, 32)
        act(v("soloE"), ind(v("solo"), oE), AF.Copy)
        act(v("Vr", 0, 32), ind(v("top"), oE), AF.Copy)
        act(ende, ind(v("iot"), oE), AF.Copy)
        act(v("SRe"), ind(v("SR"), oE), AF.Identity, -0.44, 256.0)
        act(v("d2e"), ind(v("d2"), oE), AF.Identity, -1.0)
        act(v("sf", 0, 32), endp, AF.Identity, 1.0)
        act(v("sf", 32, 64), endp, AF.Identity, 65281.0, 65280.0)
        tt(v("Vr", 32, 64), ind(v("sv"), oE), v("soloE"), A.max)
        tt(v("xm", 0, 32), ind(v("top"), oE), v("mk"), A.add)
        tt(v("xm", 32, 96, 2), ind(v("sv"), oE), v("mk"), A.add)
        tt(v("xm", 33, 96, 2), ind(v("solo"), oE), v("mk"), A.add)
        for s, (a, b) in enumerate(((0, 16), (16, 32), (32, 64), (64, 96))):
            red(col("nth", s), v("xm", a, b), A.max, True)
        for s in range(4):
            act(v("D", 64 * s, 64 * s + 64), v("Vr"), AF.Sign, col("nth", s), 1.0, col("fg", 66 * s + 64))
            ts(v("fg", 66 * s, 66 * s + 64), v("Vr"), col("nth", s), A.add, 0.0, A.not_equal)
        scan(v("rk"), v("thr"), A.mult, v("fg"), A.add, 0.0)
        ts(v("rk16", 0, 4), v("rk", 65, 264, 66), 0.5, A.mult)
        cp(v("si", 0, 32), v("SRe"))
        ts(v("si", 32, 64), v("si", 0, 32), 8, A.arith_shift_right)
        ts(v("si", 64, 96), v("si", 0, 32), 255, A.bitwise_and)
        tt(v("krow", 0, 32), ende, v("si", 32, 64), A.subtract)
        tt(v("sf", 64, 96), ende, v("d2e"), A.subtract)
        tt(v("sf", 96, 128), v("krow", 0, 32), v("si", 64, 96), A.subtract)
        tt(v("sf", 160, 192), v("sf", 64, 96), v("sf", 0, 32), A.max)
        tt(v("sf", 224, 256), v("sf", 32, 64), ende, A.add)
        tt(v("krow", 32, 64), v("sf", 160, 192), v("sf", 96, 128), A.max)
        for w in range(2):
            ts(v("k255", 32 * w, 32 * w + 32), v("krow", 32 * w, 32 * w + 32), 255.0, A.mult)
            tt(v("PK", 32 * w, 32 * w + 32), v("k255", 32 * w, 32 * w + 32), v("sf", 224, 256), A.add)
        cp(ind(v("I"), v("rk16", 0, 4)), v("PK"))
        n2 = 2 * K
        own, nxt = v("I", 0, n2), v("I", 1, n2 + 1)
        P_, W_ = v("PW", 0, 2 * n2, 2), v("PW", 1, 2 * n2, 2)

        def so(k):
            return v("so", 64 * k, 64 * k + n2)
        ts(so(0), own, 255, A.bitwise_and)
        ts(so(1), own, 0xFF00, A.bitwise_and)
        cp(col("I", n2), col("I", 0))
        ts(v("sg", 0, 2 * n2, 2), so(0), 65536.0, A.mult)
        ts(v("sg", 1, 2 * n2, 2), so(1), 256.0, A.mult)
        ts(so(2), own, 8, A.arith_shift_right, 0xFF00, A.bitwise_and)
        scan(v("PW", 1, 2 * n2 + 1), v("ones", 0, 2 * n2), A.mult, v("sg", 0, 2 * n2), A.add, -255.0 * 65536)
        ts(so(3), nxt, 16, A.arith_shift_right)
        ts(so(4), nxt, 0xFFFF, A.bitwise_and)
        tt(so(5), so(2), so(3), A.add)
        scan(v("PWx", 0, 64), v("lim", 0, 64), A.add, v("PW", 2, 130, 2), A.min, 0.0)
        scan(v("PWx", 64, 128), v("lim", 0, 64), A.add, v("PW", 1, 129, 2), A.min, 0.0)
        ts(v("oPW"), v("PWx", 15, 128, 16), 2.0 ** -16, A.mult, 255.0, A.add)
        tt(v("Vs", 128, 128 + n2), P_, so(4), A.add)
        tt(so(6), so(5), so(1), A.add)
        tt(v("Vs", 64, 64 + n2), W_, so(5), A.add)
        tt(v("Vs", 0, n2), P_, so(6), A.add)
        e0, e1, e2 = 3 * t * EW, (3 * t + 1) * EW, (3 * t + 2) * EW
        cp(ind(v("E", e2, e2 + EW), v("oPW", 0, 4)), v("Vs", 128, 192))
        cp(ind(v("E", e1, e1 + EW), v("oPW", 0, 4)), v("Vs", 64, 128))
        cp(ind(v("E", e0, e0 + EW), v("oPW", 4, 8)), v("Vs", 0, 64))
        scan(v("fill", 903, 455, -1), v("E", e2 + 448, e2, -1), A.min, v("E", e2 + 448, e2, -1), A.min, BIG)
        scan(v("EX", 448, 896), v("lim"), A.add, v("fill", 456, 904), A.min, 0.0)
        scan(v("fill", 455, 7, -1), v("E", e1 + 448, e1, -1), A.min, v("E", e0 + 448, e0, -1), A.min, BIG)
        scan(v("EX", 0, 448), v("lim"), A.add, v("fill", 8, 456), A.min, 0.0)

        def dI(k):
            return v("dI", 32 * k, 32 * k + 28)

        def dF(k):
            return v("dF", 32 * k, 32 * k + 28)
        for r in (1, 0):
            tt(dI(4 * r), v("EX", 448 * r + 15, 448 * r + 448, 16), v("cc65"), A.subtract)
            ts(dI(4 * r + 1), dI(4 * r), 255, A.bitwise_and)
            ts(dI(4 * r + 2), dI(4 * r), 8, A.arith_shift_right, 255, A.bitwise_and)
            ts(dI(4 * r + 3), dI(4 * r), 16, A.arith_shift_right)
            tt(dF(r), dI(4 * r + 2), dI(4 * r + 3), A.subtract)
        cp(v("F16"), dF(0))
        tt(dF(2), dI(5), dI(6), A.add)
        add("V", lambda: g.vector.reciprocal(ap(dF(3)), ap(dF(2))), [dF(3)], [dF(2)], 360.0)
        tt(dF(4), dF(1), dF(3), A.mult)
        tt(dF(5), dF(1), dI(1), A.add)
        ts(dI(8), dF(4), -0.498, A.add)
        tt(dF(6), dI(8), dF(2), A.mult)
        tt(dF(7), dF(5), dF(6), A.subtract)
        cp(v("G16"), dF(7))

        def zhalf(h):
            ca, cb = [], []
            for b in range(4):
                af = v("Af", 896 * h + C * b, 896 * h + C * b + C)
                ca.append(act(af, ind(v("Xh", C * b, C * b + C), v("F16", 14 * h, 14 * h + 14)), AF.Copy))
                cb.append(tt(v("Z", 896 * h + b, 896 * h + 896, 4), ind(v("Xh", C * b, C * b + C), v("G16", 14 * h, 14 * h + 14)), af, A.add))
            chain(ca)
            chain(cb)
            return quant(v(qz, C * h, C * h + C), v(sz, C * h, C * h + C), v("Z", 896 * h, 896 * h + 896))

        made = zhalf(1)
        peer = T.cores[rank ^ STEP[t]]
        rid, pid, _e = topo.addr(peer)
        arr = T.sem["arr%d" % t]
        s1 = add("G", lambda qz=qz, lq=lq, arr=arr, pid=pid, rid=rid:
                 g.remote_dma(u8(v(lq)), u8(v(qz, C, 2 * C)), arr, T.sem.sent, pid, rid, mask), [], [v(qz, C, 2 * C)], 300.0, sem="remote")
        s2 = add("G", lambda sz=sz, ls=ls, arr=arr, pid=pid, rid=rid:
                 g.remote_dma(ap(v(ls)), ap(v(sz, C, 2 * C)), arr, T.sem.sent, pid, rid, mask), [], [v(sz, C, 2 * C)], 300.0, sem="remote", after=[s1])
        add("R", None, [v(lq), v(ls)], [], ROAD, sem="arr%d" % t, count=2 * len(eng), issue=False, after=[s2])
        zhalf(0)
        mms = []
        for b in range(4):
            mms.append(mm("p%d" % b, C, wst(b)[0], wst(b)[1], v(qz, 0, C), v(sz, 0, C)))
            lastown = act(v("Hh", 448 * b, 448 * b + C), v("p%d" % b, 0, C), AF.Copy, 0.0, 2.0 ** -6)

        scan(v("tidx"), v("lim", 0, C), A.add, v("tid", 0, C), A.min, 0.0)
        ts(v("tid16"), v("tidx", 15, C, 16), 1.0 / B90, A.mult)
        cp(v("rk16", 4, 8), v("rk", 65, 264, 66))
        tt(v("Tt", 0, 32), ende, endp, A.subtract)
        act(v("Tt", 32, 64), v("Tt", 0, 32), AF.Copy)
        act(v("Tt", 64, 128), ind(v("PW"), v("rk16", 4, 8)), AF.Identity, 255.0 * 256, 2.0 ** -8)
        act(v("Tt", 128, 192), v("krow"), AF.Identity, -(2.0 ** 24), 2.0 ** 17)
        tt(v("Tt", 192, 256), v("Tt", 128, 192), v("Tt", 0, 64), A.add)
        tt(v("Tt", 256, 320), v("Tt", 192, 256), v("Tt", 64, 128), A.add)
        act(v("RR", 0, C), ind(v("Tt", 256, 288), v("tid16")), AF.Copy)
        act(v("RR", C, 2 * C), ind(v("Tt", 288, 320), v("tid16")), AF.Copy)
        scan(v("RX"), v("lim"), A.add, v("RR"), A.min, 0.0)

        def eI(k):
            return v("eI", 32 * k, 32 * k + 28)
        cp(eI(0), v("RX", 15, 448, 16))
        ts(eI(1), eI(0), 17, A.arith_shift_right)
        ts(eI(2), eI(0), 8, A.arith_shift_right, 511, A.bitwise_and)
        ts(eI(3), eI(0), 255, A.bitwise_and)
        tt(eI(4), eI(1), v("ccol"), A.subtract)
        ts(eI(5), eI(4), 0.0, A.max, 256.0, A.mult)
        tt(eI(6), eI(2), eI(4), A.subtract)
        tt(eI(7), eI(5), eI(3), A.min)
        tt(eI(8), eI(6), eI(7), A.add)
        cp(v("pq16"), eI(8))
        if t == ROUNDS - 1:
            act(v("olr"), ind(v("iot"), v("F16")), AF.Copy)
            dma("Y", lambda: g.sync.dma_start(T.ol[:], T.olr[0:128:16, :]), [], [v("olr")])
        for b in range(4):
            mms.append(mm("p%d" % (4 + b), C, wst(b)[0], wst(b)[1], v(lq), v(ls)))
        chain(mms)
        z = []
        for b in range(4):
            hb, hw = v("Hh", 448 * b + C, 448 * b + 2 * C), v("Hh", 448 * b, 448 * b + 448)
            if b == 1:
                z.append(ts(hb, v("p%d" % (4 + b), 0, C), 2.0 ** -6, A.mult))
            else:
                z.append(act(hb, v("p%d" % (4 + b), 0, C), AF.Copy, 0.0, 2.0 ** -6))
            z.append(act(v("Ap", C * b, C * b + C), ind(hw, v("pq16", 0, 14)), AF.Copy))
            z.append(tt(v("ss", C * b, C * b + C), ind(hw, v("pq16", 14, 28)), v("Ap", C * b, C * b + C), A.add))
            z.append(tt(v(Xn, b, 4 * C, 4), v("ss", C * b, C * b + C), v(X, b, 4 * C, 4), A.add))
        chain([z[k] for k in (2, 6, 3, 10, 7, 14, 11, 15)])
        chain([lastown] + [z[k] for k in (0, 8, 1, 5, 12, 9, 13)])

    quant(v("qx"), v("sx"), v("X%d" % (ROUNDS % 2)))
    mm("p0", C, v("vq"), v("vs"), v("qx"), v("sx"))
    dma("Y", lambda: g.sync.dma_start(T.oc[:], u8(v("qx"))), [], [v("qx")])
    for k in range(4):
        dma("S" if k < 2 else "Y", lambda k=k: Q["S" if k < 2 else "Y"].dma_start(T.osc[4 * k:4 * k + 4, :], T.sx[32 * k:32 * k + 4, :]), [], [v("sx")])
    cp(v("yb"), v("p0", 0, C))
    dma("S", lambda: g.scalar.dma_start(T.y[:], T.yb[:]), [], [v("yb")])

    def cells(x):
        return np.arange(1) if SCRATCH[x[0]][0] == "psum" else np.arange(x[1], x[2], x[3])

    lastw, readers = {}, {}
    for i, o in enumerate(ops):
        deps = set()
        for x in o["r"] + o["w"]:
            if x[0] not in lastw:
                lastw[x[0]] = np.full(SCRATCH[x[0]][1][1], -1)
                readers[x[0]] = []
            deps |= set(int(d) for d in np.unique(lastw[x[0]][cells(x)]))
        for x in o["w"]:
            cs = set(cells(x).tolist())
            deps |= set(j for j, c2 in readers[x[0]] if cs & c2)
            readers[x[0]] = [(j, c2 - cs) for j, c2 in readers[x[0]] if c2 - cs]
        for x in o["r"]:
            if SCRATCH[x[0]][0] == "psum":
                deps |= set(j for j, c2 in readers[x[0]] if ops[j]["eng"] != o["eng"])
        deps.discard(-1)
        deps.discard(i)
        o["deps"] = deps
        for x in o["w"]:
            lastw[x[0]][cells(x)] = i
        for x in o["r"]:
            readers[x[0]].append((i, set(cells(x).tolist())))

    n = len(ops)
    pre = [dict([(d, 0.0) for d in o["after"]] + [(d, ops[d]["lat"] + WAKE) for d in o["deps"]]) for o in ops]
    post = [{} for o in ops]
    for i in range(n):
        for d, w in pre[i].items():
            post[d][i] = w

    def place(before, behind, rank_of, gaps):
        need = [len(b) for b in before]
        ready = [i for i in range(n) if not need[i]]
        at, busy = {}, {}
        while ready:
            i = max(ready, key=rank_of)
            ready.remove(i)
            c = ops[i]["cost"]
            s = max([at[d] + ops[d]["cost"] + w for d, w in before[i].items()] + [0.0 if before is pre else ops[i]["lat"]])
            if gaps:
                line = busy.setdefault(ops[i]["eng"], [])
                for a, b in line:
                    if s + c <= a:
                        break
                    s = max(s, b)
                line.append((s, s + c))
                line.sort()
            at[i] = s
            for j in behind[i]:
                need[j] -= 1
                if not need[j]:
                    ready.append(j)
        return at

    back = place(post, pre, lambda j: j, False)
    start, best = None, None
    for turn in range(PASSES):
        fwd = place(pre, post, lambda j: (back[j] + ops[j]["cost"], -j), True)
        end = max(fwd[j] + ops[j]["cost"] + ops[j]["lat"] for j in range(n))
        if best is None or end < best:
            start, best = fwd, end
        back = place(post, pre, lambda j: (fwd[j] + ops[j]["cost"], j), True)
    order = sorted(range(n), key=lambda j: (start[j], j))

    seq, known, clock, waited = {}, {}, {}, set()
    for i in order:
        o = ops[i]
        o["key"] = o["sem"] if o["sem"] else o["eng"]
        seq[o["key"]] = seq.get(o["key"], 0) + 1
        o["seq"] = seq[o["key"]]
        kn = known.setdefault(o["eng"], {})
        o["waits"] = []
        if o["issue"]:
            for d in sorted(o["deps"], key=lambda j: -start[j]):
                p = ops[d]
                if kn.get(p["key"], 0) < p["seq"]:
                    o["waits"].append(d)
                    waited.add(d)
                    for k2, s2 in clock[d].items():
                        kn[k2] = max(kn.get(k2, 0), s2)
        clock[i] = dict(kn)
        clock[i][o["key"]] = o["seq"]
    total = {}
    for i in order:
        o = ops[i]
        if not o["sem"] and i in waited:
            total[o["eng"]] = total.get(o["eng"], 0) + 1
            o["count"] = total[o["eng"]]
    for i in order:
        o = ops[i]
        if not o["issue"]:
            continue
        for d in o["waits"]:
            p = ops[d]
            Q[o["eng"]].wait_ge(T.sem[p["sem"] if p["sem"] else "c" + p["eng"]], p["count"])
        ins = o["fn"]()
        if o["sem"] == "remote":
            continue
        if o["sem"]:
            ins.then_inc(T.sem[o["sem"]], 16)
        elif i in waited:
            ins.then_inc(T.sem["c" + o["eng"]], 1)
    g.wait_ge(T.sem.sent, 2 * len(eng) * ROUNDS)
    for i in order:
        o = ops[i]
        if o["sem"] and o["sem"][:2] == "dm" and i not in waited:
            g.wait_ge(T.sem[o["sem"]], 16)
